import numpy as np
import ml_dtypes


def mxq(x, axis, fmt="e4m3"):
    dtype, down = {"e4m3": (ml_dtypes.float8_e4m3fn, 7), "e5m2": (ml_dtypes.float8_e5m2, 14)}[fmt]
    v = np.moveaxis(np.asarray(x, np.float32).astype(ml_dtypes.bfloat16).astype(np.float64), axis, -1)
    blocks = v.reshape(v.shape[:-1] + (-1, 32))
    amax = np.abs(blocks).max(-1, keepdims=True)
    byte = np.maximum(np.where(amax > 0, np.frexp(amax)[1] - 1 + 127, 0) - down, 1)
    scale = np.exp2(byte - 127.0)
    codes = (blocks / scale).astype(np.float32).astype(dtype).astype(np.float64)
    return np.moveaxis((codes * scale).reshape(v.shape), -1, axis)


WIDE = False


def mx_kscale(k):
    if not WIDE:
        return np.ones(k)
    levels = np.array([10, -10, 5, -5, 0])
    if k % 512:
        return np.exp2(np.random.permutation(np.resize(levels, k // 32))).repeat(32)
    a = np.empty((k // 512, 16))
    for p in range(k // 512):
        a[p, :8] = np.random.permutation(np.resize(levels, 8))
        for g in range(8):
            far = levels[np.abs(levels - a[p, g]) >= 10]
            a[p, g + 8] = far[np.random.randint(len(far))]
    return np.exp2(a.ravel()).repeat(32)


BF16 = ml_dtypes.bfloat16


def bf(x):
    return np.asarray(x, np.float32).astype(BF16)


def f64(x):
    return np.asarray(x).astype(np.float64)


E2M1 = np.array([0.0, 0.5, 1.0, 1.5, 2.0, 3.0, 4.0, 6.0, -0.0, -0.5, -1.0, -1.5, -2.0, -3.0, -4.0, -6.0])


def pack_weight(w, fmt):
    k, n = w.shape
    w = f64(bf(w)).reshape(k // 32, 32, n)
    amax = np.abs(w).max(1)
    if fmt == "e4m3":
        byte = np.frexp(amax)[1] - 1 + 127 - 7
    else:
        mant, ex = np.frexp(amax / 6.0)
        byte = np.where(mant > 0.5, ex, ex - 1) + 127
    byte = np.clip(np.where(amax > 0, byte, 1), 1, 254)
    scaled = (w * np.exp2(127.0 - byte)[:, None, :]).reshape(k, n).astype(np.float32)
    by_word = np.ascontiguousarray(scaled.reshape(k // 512, 128, 4, n).transpose(0, 1, 3, 2))
    if fmt == "e4m3":
        words = by_word.astype(ml_dtypes.float8_e4m3fn).view(np.uint8)
    else:
        c = by_word.astype(ml_dtypes.float4_e2m1fn).view(np.uint8) & 0xF
        words = c[..., 0::2] | (c[..., 1::2] << 4)
    return np.ascontiguousarray(words), np.ascontiguousarray(byte.astype(np.uint8).reshape(k // 512, 16, n))


def unpack_weight(words, scales, fmt):
    g, p, n, _ = words.shape
    if fmt == "e4m3":
        vals = np.ascontiguousarray(words).view(ml_dtypes.float8_e4m3fn).astype(np.float64)
    else:
        nib = np.empty((g, p, n, 4), np.uint8)
        nib[..., 0::2] = words & 0xF
        nib[..., 1::2] = words >> 4
        vals = E2M1[nib]
    vals = vals * np.repeat(np.exp2(scales.astype(np.float64) - 127.0), 8, axis=1)[..., None]
    return vals.transpose(0, 1, 3, 2).reshape(g * 512, n)
def pack4(w):
    words, scales = pack_weight(w, "e2m1")
    return words.reshape(words.shape[0], 128, -1), scales


def unpack4(words, scales):
    return unpack_weight(words.reshape(words.shape[0], 128, -1, 2), scales, "e2m1")


T, D, H, N = 1024, 1024, 4, 32
TWO = 2
C = H * TWO * N
SLOTS = N * N


def draw0():
    s = mx_kscale(D)
    t = mx_kscale(SLOTS)
    x = bf(np.random.standard_normal((T, D)) * s)
    wk_words, wk_scales = pack4(np.random.standard_normal((D, C)) * 1.5 / np.sqrt(D) / s[:, None])
    slot_gain = bf(np.random.standard_normal(SLOTS) * np.sqrt(SLOTS) * t)
    values_words, values_scales = pack4(np.random.standard_normal((SLOTS, D)) * 2.0 / np.sqrt(SLOTS) / t[:, None])
    wg_words, wg_scales = pack4(np.random.standard_normal((D, D)) * 1.5 / np.sqrt(D) / s[:, None])
    return {
        "x": x,
        "wk_words": wk_words,
        "wk_scales": wk_scales,
        "slot_gain": slot_gain,
        "values_words": values_words,
        "values_scales": values_scales,
        "wg_words": wg_words,
        "wg_scales": wg_scales,
    }


def softmax(v):
    e = np.exp(v - v.max(-1, keepdims=True))
    return e / e.sum(-1, keepdims=True)


def product_key_weights(sc):
    p = softmax(sc)
    p1 = p[:, :, 0, :]
    p2 = p[:, :, 1, :]
    w = np.sum(p1[:, :, :, None] * p2[:, :, None, :], axis=1)
    return w.reshape(w.shape[0], SLOTS)


def core(x, wk_words, wk_scales, slot_gain, values_words, values_scales, wg_words, wg_scales):
    xq = mxq(f64(x), 1, "e4m3")
    sc = (xq @ unpack4(wk_words, wk_scales)).reshape(x.shape[0], H, TWO, N)
    w = product_key_weights(sc)
    wg_slots = w * f64(slot_gain)[None, :]
    mem = mxq(wg_slots, 1, "e4m3") @ unpack4(values_words, values_scales)
    a = xq @ unpack4(wg_words, wg_scales)
    gate = a * (1.0 / (1.0 + np.exp(-a)))
    return mem * gate


def e4m3fn_bytes(y):
    return np.clip(np.asarray(y, np.float64), -448.0, 448.0).astype(np.float32).astype(ml_dtypes.float8_e4m3fn).view(np.uint8)


def e4m3fn_values(b):
    return np.asarray(b, np.uint8).view(ml_dtypes.float8_e4m3fn).astype(np.float64)


def setup_inputs():
    d = draw0()
    x0 = np.asarray(d['x']).astype(np.float64)
    s = (np.max(np.abs(x0), axis=(0,), keepdims=True) / 448.0).astype(np.float32)
    out = {}
    for k, v in d.items():
        if k == 'x':
            out['x_bytes'] = e4m3fn_bytes(x0 / s.astype(np.float64))
            out['x_scale'] = s
        else:
            out[k] = v
    return out


def reference(x_bytes, x_scale, wk_words, wk_scales, slot_gain, values_words, values_scales, wg_words, wg_scales):
    return core(e4m3fn_values(x_bytes) * x_scale.astype(np.float64), wk_words, wk_scales, slot_gain, values_words, values_scales, wg_words, wg_scales)

@@ -1,0 +1,343 @@
+from contextlib import ExitStack
+
+import concourse.mybir as mybir
+from concourse.masks import make_identity
+
+T, D, H, N = 1024, 1024, 4, 32
+C = H * 2 * N
+SLOTS = N * N
+FLOPS = 2 * T * D * C + 2 * T * SLOTS * D + 2 * T * D * D
+
+P = 128
+PACK = 4
+PASSES = 2
+HALVES = 2
+Q = 4
+GROUPS = 16
+
+F32 = mybir.dt.float32
+BF16 = mybir.dt.bfloat16
+I32 = mybir.dt.int32
+U32 = mybir.dt.uint32
+U8 = mybir.dt.uint8
+FP8 = mybir.dt.float8_e4m3fn
+E4M3X4 = mybir.dt.float8_e4m3fn_x4
+E2M1X4 = mybir.dt.float4_e2m1fn_x4
+ADD = mybir.AluOpType.add
+SUB = mybir.AluOpType.subtract
+MUL = mybir.AluOpType.mult
+MAX = mybir.AluOpType.max
+AX = mybir.AxisListType.X
+EXP = mybir.ActivationFunctionType.Exp
+SILU = mybir.ActivationFunctionType.Silu
+
+
+def tile_productkeysoftmemoryplus_w4_kernel(
+    tc, x_bytes, x_scale, wk_words, wk_scales, slot_gain, values_words, values_scales, wg_words, wg_scales, out
+):
+    nc = tc.nc
+    with ExitStack() as ctx:
+        keep = ctx.enter_context(tc.tile_pool(name="keep", bufs=1))
+        work = ctx.enter_context(tc.tile_pool(name="work", bufs=4))
+        pst = ctx.enter_context(tc.psum_pool(name="pst", bufs=2))
+        psm = ctx.enter_context(tc.psum_pool(name="psm", bufs=6))
+
+        ctx.enter_context(tc.manual_schedule())
+        x_view = x_bytes.rearrange("(s r q) d -> s r q d", s=HALVES, q=Q)
+        out_view = out.rearrange("(s r q) d -> s r q d", s=HALVES, q=Q)
+
+        warm = keep.tile([P, 1], F32, name="warm")
+        nc.vector.memset(warm[:], 0.0)
+        nc.scalar.activation(out=warm[:], in_=warm[:], func=EXP)
+        xb = [keep.tile([P, Q, D], U8, name=f"xb{s}", align_bytes=64) for s in range(HALVES)]
+        scale_col = keep.tile([P, 8], F32, name="scale_col")
+        nc.sync.dma_start(out=scale_col[:], in_=x_scale.rearrange("o (m p) -> p (o m)", p=P))
+        for q in range(Q):
+            nc.sync.dma_start(out=xb[0][:, q, :], in_=x_view[0][:, q, :])
+
+        ident = keep.tile([P, P], F32, name="ident", align_bytes=64)
+        make_identity(nc, ident[:])
+
+        def load_weight(words, scales, n, name):
+            w = keep.tile([P, PASSES, 2 * n], U8, name=name + "_w", align_bytes=64)
+            sc = keep.tile([P, PASSES, n], U8, name=name + "_s", align_bytes=64)
+            nc.vector.memset(sc[:].rearrange("p g n -> p (g n)").bitcast(I32), 0)
+            nc.sync.dma_start(
+                out=w[:].rearrange("p g n -> p (g n)").bitcast(I32).rearrange("p (g n) -> p g n", g=PASSES),
+                in_=words.rearrange("g p n -> (g p) n").bitcast(I32).rearrange("(g p) n -> p g n", g=PASSES),
+            )
+            s32 = sc[:].rearrange("p g n -> p (g n)").bitcast(I32).rearrange("p (g n) -> p g n", g=PASSES)
+            src = scales.rearrange("g r n -> (g r) n").bitcast(I32).rearrange("(g r) n -> r g n", g=PASSES)
+            for quad in range(4):
+                nc.sync.dma_start(out=s32[32 * quad : 32 * quad + 4], in_=src[4 * quad : 4 * quad + 4])
+            return w, sc
+
+        wk_w, wk_s = load_weight(wk_words, wk_scales, C, "wk")
+        nc.sync.dma_start(out=xb[1][:], in_=x_view[1])
+        wg_w, wg_s = load_weight(wg_words, wg_scales, D, "wg")
+        gain = keep.tile([P, N], BF16, name="gain")
+        for q in range(Q):
+            nc.sync.dma_start(out=gain[32 * q : 32 * q + 32, :], in_=slot_gain.rearrange("(i j) -> i j", j=N))
+        v_w, v_s = load_weight(values_words, values_scales, D, "vl")
+
+        left = [keep.tile([P, GROUPS, Q, N], F32, name=f"left{s}") for s in range(HALVES)]
+        right = [keep.tile([P, GROUPS, 8, N], F32, name=f"right{s}") for s in range(HALVES)]
+        for s in range(HALVES):
+            eng = nc.vector if s == 0 else nc.gpsimd
+            eng.memset(left[s][:], 0.0)
+            eng.memset(right[s][:], 0.0)
+
+        scl = keep.tile([P, D], F32, name="scl")
+        for b in range(2):
+            ps = psm.tile([P, 512], F32, name="mm")
+            for m in range(4):
+                nc.tensor.transpose(
+                    ps[:, 128 * m : 128 * m + 128], scale_col[:, 4 * b + m : 4 * b + m + 1].to_broadcast([P, P]), ident[:]
+                )
+            if b == 0:
+                nc.scalar.copy(out=scl[:, 0:512], in_=ps[:])
+            else:
+                nc.vector.tensor_copy(out=scl[:, 512:1024], in_=ps[:])
+
+        S = {}
+
+        def xs(s, q):
+            t = work.tile([P, D], BF16, name="xs", align_bytes=64)
+            nc.vector.tensor_tensor(out=t[:], in0=xb[s][:, q, :].bitcast(FP8), in1=scl[:], op=MUL)
+            S["xs", s, q] = t
+
+        def xt(s, q):
+            xw = S["xs", s, q][:].bitcast(F32)
+            ps = pst.tile([P, PASSES, 2, P], F32, name="tp")
+            for g in range(PASSES):
+                for u in range(2):
+                    nc.tensor.transpose(ps[:, g, u, :], xw[:, 256 * g + u : 256 * (g + 1) : 2], ident[:])
+            xg = work.tile([P, PASSES, P, PACK], BF16, name="xg", align_bytes=64)
+            nc.scalar.copy(
+                out=xg[:].rearrange("p g r t -> p (g r t)").bitcast(F32).rearrange("p (g r u) -> p g r u", g=PASSES, u=2),
+                in_=ps[:].rearrange("p g u r -> p g r u"),
+            )
+            S["xg", s, q] = xg
+
+        def quant(src, key):
+            c = keep.tile([P, PASSES, P], U32, name="c_" + "_".join(str(k) for k in key), align_bytes=64)
+            sc = keep.tile([P, PASSES, P], U8, name="s_" + "_".join(str(k) for k in key), align_bytes=64)
+            nc.vector.quantize_mx(
+                out=c[:].rearrange("p g r -> p (g r)").bitcast(E4M3X4),
+                scales=sc[:].rearrange("p g r -> p (g r)"),
+                in_=src[:].rearrange("p g r t -> p (g r t)"),
+            )
+            S[key] = (c, sc)
+
+        def qx(s, q):
+            quant(S["xg", s, q], ("x", s, q))
+
+        def mx(ps, key, w, wsc, n0, n):
+            codes, scales = S[key]
+            for g in range(PASSES):
+                nc.tensor.matmul_mx(
+                    out=ps,
+                    lhsT=codes[:, g, :].bitcast(E4M3X4),
+                    lhsT_scale=scales[:, g, :],
+                    rhs=w[:, g, 2 * n0 : 2 * (n0 + n)].bitcast(E2M1X4),
+                    rhs_scale=wsc[:, g, n0 : n0 + n],
+                    start=(g == 0),
+                    stop=(g == PASSES - 1),
+                )
+
+        for s in range(HALVES):
+            S["e", s] = keep.tile([P, H, Q, 2, N], F32, name=f"e{s}")
+            S["z", s] = keep.tile([P, H, Q, 2], F32, name=f"z{s}")
+
+        def sc(s, k):
+            ps = psm.tile([P, 2, C], F32, name="mm")
+            for m in range(2):
+                for n0 in (0, 128):
+                    mx(ps[:, m, n0 : n0 + 128], ("x", s, 2 * k + m), wk_w, wk_s, n0, 128)
+            S["sc", s, k] = ps
+
+        def mxs(s, k):
+            ps = S["sc", s, k]
+            top = work.tile([P, 2, H, 2], F32, name="top")
+            nc.vector.tensor_reduce(
+                out=top[:].rearrange("p k h a -> p (k h a)"),
+                in_=ps[:].rearrange("p k (h a n) -> p (k h a) n", h=H, a=2),
+                axis=AX,
+                op=MAX,
+            )
+            S["top", s, k] = top
+
+        def sub(s, q):
+            e = S["e", s]
+            nc.vector.tensor_tensor(
+                out=e[:, :, q, :, :],
+                in0=S["sc", s, q // 2][:, q % 2, :].rearrange("p (h a n) -> p h a n", h=H, a=2),
+                in1=S["top", s, q // 2][:, q % 2, :, :].unsqueeze(3).to_broadcast([P, H, 2, N]),
+                op=SUB,
+            )
+            nc.scalar.activation(out=e[:, :, q, :, :], in_=e[:, :, q, :, :], func=EXP)
+
+        def sm(s, q):
+            nc.vector.tensor_reduce(out=S["z", s][:, :, q, :], in_=S["e", s][:, :, q, :, :], axis=AX, op=ADD)
+
+        def norm(s):
+            e, z = S["e", s], S["z", s]
+            zz = work.tile([P, H, Q], F32, name="zz")
+            nc.vector.tensor_tensor(out=zz[:], in0=z[:, :, :, 0], in1=z[:, :, :, 1], op=MUL)
+            rz = work.tile([P, H, Q], F32, name="rz")
+            nc.vector.reciprocal(out=rz[:], in_=zz[:])
+            first = e[:, :, :, 0, :].rearrange("p h q n -> p (h q) n")
+            nc.vector.tensor_tensor(
+                out=first, in0=first, in1=rz[:].rearrange("p h q -> p (h q)").unsqueeze(2).to_broadcast([P, H * Q, N]), op=MUL
+            )
+            park = out[768 + 128 * s : 896 + 128 * s, :]
+            nc.sync.dma_start(out=park, in_=e[:].rearrange("p h q a n -> p (h q a n)"))
+            for r in range(8):
+                src = park.rearrange("(g r) (c a n) -> r c g a n", r=8, a=2, n=N)[r][:, :, 1, :]
+                nc.sync.dma_start(out=right[s][16 * r : 16 * r + 16, :, r, :], in_=src)
+            for q in range(Q):
+                src = park.rearrange("(g r) (h q a n) -> r h g q a n", r=8, h=H, q=Q, a=2)[:, :, :, q, 0, :]
+                nc.sync.dma_start(out=left[s][q : P : Q, :, q, :], in_=src.rearrange("r h g n -> (r h) g n"))
+
+        def gate(s, q, b):
+            if b == 0:
+                S["gate", s, q] = keep.tile([P, D], F32, name=f"gate{s}{q}")
+            ps = psm.tile([P, 512], F32, name="mm")
+            mx(ps[:], ("x", s, q), wg_w, wg_s, 512 * b, 512)
+            nc.scalar.activation(out=S["gate", s, q][:, 512 * b : 512 * b + 512], in_=ps[:], func=SILU)
+
+        for s in range(HALVES):
+            S["wt", s] = keep.tile([P, 16, P, 2], BF16, name=f"wt{s}", align_bytes=64)
+            S["u1", s] = keep.tile([P, 2, Q, N, 8], F32, name=f"u1{s}")
+
+        def prod(s, b):
+            ps = psm.tile([P, 2, 8 * N], F32, name="mm")
+            for k in range(2):
+                grp = 2 * b + k
+                nc.tensor.matmul(
+                    out=ps[:, k, :],
+                    lhsT=left[s][:, grp, :, :].rearrange("p q n -> p (q n)"),
+                    rhs=right[s][:, grp, :, :].rearrange("p r n -> p (r n)"),
+                    start=True,
+                    stop=True,
+                )
+            S["pr", s, b] = ps
+
+        def gn(s, b):
+            nc.vector.tensor_tensor(
+                out=S["wt", s][:, :, 16 * b : 16 * b + 16, :],
+                in0=S["pr", s, b][:].rearrange("p k (r w e) -> p w (k r) e", r=8, e=2),
+                in1=gain[:].rearrange("p (w e) -> p w e", e=2).unsqueeze(2).to_broadcast([P, 16, 16, 2]),
+                op=MUL,
+            )
+
+        def t1(s, b, vec=False):
+            words = S["wt", s][:].rearrange("p w r e -> p (w r e)").bitcast(F32)
+            u, jh = b // 2, b % 2
+            ps = pst.tile([P, 4, P], F32, name="tp")
+            for c in range(4):
+                w = 2 * (4 * jh + c) + u
+                nc.tensor.transpose(ps[:, c, :], words[:, 128 * w : 128 * w + 128], ident[:])
+            dst = S["u1", s][:, u, :, :, 4 * jh : 4 * jh + 4].rearrange("p q i c -> p (q i) c")
+            src = ps[:].rearrange("p c m -> p m c")
+            if vec:
+                nc.vector.tensor_copy(out=dst, in_=src)
+            else:
+                nc.scalar.copy(out=dst, in_=src)
+
+        def t2(s, q):
+            ps = pst.tile([P, PASSES, 2, P], F32, name="tp")
+            for g in range(PASSES):
+                for u in range(2):
+                    nc.tensor.transpose(
+                        ps[:, g, u, :], S["u1", s][:, u, q, 16 * g : 16 * g + 16, :].rearrange("p i j -> p (i j)"), ident[:]
+                    )
+            ug = work.tile([P, PASSES, P, PACK], BF16, name="xg", align_bytes=64)
+            nc.scalar.copy(
+                out=ug[:].rearrange("p g r t -> p (g r t)").bitcast(F32).rearrange("p (g r u) -> p g r u", g=PASSES, u=2),
+                in_=ps[:].rearrange("p g u r -> p g r u"),
+            )
+            S["ug", s, q] = ug
+
+        def qu(s, q):
+            quant(S["ug", s, q], ("u", s, q))
+
+        def val(s, q, b):
+            ps = psm.tile([P, 512], F32, name="mm")
+            mx(ps[:], ("u", s, q), v_w, v_s, 512 * b, 512)
+            S["mem", s, q, b] = ps
+
+        def fin(s, q, b):
+            if b == 0:
+                S["res", s, q] = work.tile([P, D], F32, name="res")
+            sl = slice(512 * b, 512 * b + 512)
+            nc.vector.tensor_tensor(out=S["res", s, q][:, sl], in0=S["mem", s, q, b][:], in1=S["gate", s, q][:, sl], op=MUL)
+            if b == 1:
+                nc.sync.dma_start(out=out_view[s][:, q, :], in_=S["res", s, q][:])
+
+        A, B = 0, 1
+        xs(A, 0); xt(A, 0)
+        xs(A, 1); xt(A, 1)
+        xs(A, 2); qx(A, 0); xt(A, 2)
+        xs(A, 3); qx(A, 1); xt(A, 3)
+        sc(A, 0)
+        qx(A, 2)
+        mxs(A, 0); sub(A, 0); sub(A, 1)
+        qx(A, 3)
+        sc(A, 1)
+        sm(A, 0); mxs(A, 1); sub(A, 2); sm(A, 1); sub(A, 3)
+        xs(B, 0)
+        sm(A, 2); sm(A, 3)
+        norm(A)
+        gate(A, 0, 0); gate(A, 0, 1)
+        xt(B, 0)
+        xs(B, 1); gate(A, 1, 0); gate(A, 1, 1); xt(B, 1)
+        qx(B, 0)
+        xs(B, 2); gate(A, 2, 0); gate(A, 2, 1); xt(B, 2)
+        qx(B, 1)
+        sc(B, 0)
+        xs(B, 3); gate(A, 3, 0); gate(A, 3, 1); xt(B, 3)
+        qx(B, 2)
+        mxs(B, 0); sub(B, 0); sub(B, 1)
+        qx(B, 3)
+        sc(B, 1)
+        prod(A, 0); sm(B, 0); mxs(B, 1); sub(B, 2); sm(B, 1); sub(B, 3)
+        gn(A, 0)
+        prod(A, 1); sm(B, 2); sm(B, 3); norm(B); gn(A, 1)
+        for b in range(2, 8):
+            prod(A, b); gn(A, b)
+        gate(B, 0, 0); gate(B, 0, 1)
+        for b in range(4):
+            t1(A, b)
+        gate(B, 1, 0); gate(B, 1, 1)
+        prod(B, 0); gn(B, 0)
+        gate(B, 2, 0); gate(B, 2, 1)
+        t2(A, 0)
+        prod(B, 1); gn(B, 1); qu(A, 0)
+        val(A, 0, 0); val(A, 0, 1)
+        prod(B, 2); gn(B, 2); fin(A, 0, 0); fin(A, 0, 1)
+        t2(A, 1)
+        gate(B, 3, 0); gate(B, 3, 1)
+        prod(B, 3); gn(B, 3); qu(A, 1)
+        val(A, 1, 0); val(A, 1, 1)
+        prod(B, 4); gn(B, 4); fin(A, 1, 0); fin(A, 1, 1)
+        t2(A, 2)
+        prod(B, 5); gn(B, 5); qu(A, 2)
+        prod(B, 6); gn(B, 6)
+        prod(B, 7); gn(B, 7)
+        val(A, 2, 0); val(A, 2, 1)
+        t2(A, 3)
+        t1(B, 0); t1(B, 1, True)
+        qu(A, 3); fin(A, 2, 0); fin(A, 2, 1)
+        t1(B, 2); t1(B, 3, True)
+        val(A, 3, 0); val(A, 3, 1)
+        t2(B, 0); qu(B, 0)
+        t2(B, 1); fin(A, 3, 0); fin(A, 3, 1); qu(B, 1)
+        val(B, 0, 0); val(B, 0, 1)
+        t2(B, 2); fin(B, 0, 0); qu(B, 2); fin(B, 0, 1)
+        val(B, 1, 0); val(B, 1, 1)
+        t2(B, 3); fin(B, 1, 0); qu(B, 3); fin(B, 1, 1)
+        val(B, 2, 0); val(B, 2, 1)
+        fin(B, 2, 0); fin(B, 2, 1)
+        val(B, 3, 0); val(B, 3, 1)
+        fin(B, 3, 0); fin(B, 3, 1)

@@ -11,9 +11,9 @@ FLOPS = 2 * T * D * C + 2 * T * SLOTS * D + 2 * T * D * D
 P = 128
 PACK = 4
 PASSES = 2
-HALVES = 2
+NT = 8
 Q = 4
-GROUPS = 16
+BATCHES = ((0, 1), (2, 3, 4), (5, 6, 7))
 
 F32 = mybir.dt.float32
 BF16 = mybir.dt.bfloat16
@@ -29,6 +29,7 @@ MUL = mybir.AluOpType.mult
 MAX = mybir.AluOpType.max
 AX = mybir.AxisListType.X
 EXP = mybir.ActivationFunctionType.Exp
+COPY = mybir.ActivationFunctionType.Copy
 SILU = mybir.ActivationFunctionType.Silu
 
 
@@ -38,22 +39,23 @@ def tile_productkeysoftmemoryplus_w4_kernel(
     nc = tc.nc
     with ExitStack() as ctx:
         keep = ctx.enter_context(tc.tile_pool(name="keep", bufs=1))
-        work = ctx.enter_context(tc.tile_pool(name="work", bufs=4))
+        work = ctx.enter_context(tc.tile_pool(name="work", bufs=6))
         pst = ctx.enter_context(tc.psum_pool(name="pst", bufs=2))
         psm = ctx.enter_context(tc.psum_pool(name="psm", bufs=6))
-
         ctx.enter_context(tc.manual_schedule())
-        x_view = x_bytes.rearrange("(s r q) d -> s r q d", s=HALVES, q=Q)
-        out_view = out.rearrange("(s r q) d -> s r q d", s=HALVES, q=Q)
+        S = {}
 
         warm = keep.tile([P, 1], F32, name="warm")
         nc.vector.memset(warm[:], 0.0)
         nc.scalar.activation(out=warm[:], in_=warm[:], func=EXP)
-        xb = [keep.tile([P, Q, D], U8, name=f"xb{s}", align_bytes=64) for s in range(HALVES)]
+
+        x_view = x_bytes.rearrange("(n p) d -> p n d", p=P)
+        xb = [keep.tile([P, k, D], U8, name=f"xb{k}_{n}", align_bytes=64) for n, k in ((0, 1), (1, 3), (4, 4))]
+        X_AT = {n: (xb[0] if n == 0 else xb[1] if n < 4 else xb[2], n - (0 if n == 0 else 1 if n < 4 else 4)) for n in range(NT)}
         scale_col = keep.tile([P, 8], F32, name="scale_col")
         nc.sync.dma_start(out=scale_col[:], in_=x_scale.rearrange("o (m p) -> p (o m)", p=P))
-        for q in range(Q):
-            nc.sync.dma_start(out=xb[0][:, q, :], in_=x_view[0][:, q, :])
+        nc.sync.dma_start(out=xb[0][:], in_=x_view[:, 0:1, :])
+        nc.sync.dma_start(out=xb[1][:], in_=x_view[:, 1:4, :])
 
         ident = keep.tile([P, P], F32, name="ident", align_bytes=64)
         make_identity(nc, ident[:])
@@ -73,19 +75,31 @@ def tile_productkeysoftmemoryplus_w4_kernel(
             return w, sc
 
         wk_w, wk_s = load_weight(wk_words, wk_scales, C, "wk")
-        nc.sync.dma_start(out=xb[1][:], in_=x_view[1])
         wg_w, wg_s = load_weight(wg_words, wg_scales, D, "wg")
+        nc.sync.dma_start(out=xb[2][:], in_=x_view[:, 4:8, :])
         gain = keep.tile([P, N], BF16, name="gain")
-        for q in range(Q):
-            nc.sync.dma_start(out=gain[32 * q : 32 * q + 32, :], in_=slot_gain.rearrange("(i j) -> i j", j=N))
         v_w, v_s = load_weight(values_words, values_scales, D, "vl")
 
-        left = [keep.tile([P, GROUPS, Q, N], F32, name=f"left{s}") for s in range(HALVES)]
-        right = [keep.tile([P, GROUPS, 8, N], F32, name=f"right{s}") for s in range(HALVES)]
-        for s in range(HALVES):
-            eng = nc.vector if s == 0 else nc.gpsimd
-            eng.memset(left[s][:], 0.0)
-            eng.memset(right[s][:], 0.0)
+        mask = keep.tile([P, Q], F32, name="mask")
+        perm = keep.tile([P, P], F32, name="perm", align_bytes=64)
+        place = {n: (c, 4 * k) for c, tiles in enumerate(BATCHES) for k, n in enumerate(tiles)}
+        left, left_c, right = [], [], []
+        for c, tiles in enumerate(BATCHES):
+            left.append(keep.tile([P, 4 * len(tiles), Q, N], F32, name=f"left{c}"))
+            left_c.append(keep.tile([P, 4 * len(tiles), N], F32, name=f"left_c{c}"))
+            right.append(keep.tile([P, 4 * len(tiles), 8, N], F32, name=f"right{c}"))
+            nc.gpsimd.memset(right[c][:], 0.0)
+        for q in range(Q):
+            nc.gpsimd.dma_start(out=gain[32 * q : 32 * q + 32, :], in_=slot_gain.rearrange("(i j) -> i j", j=N))
+        nc.vector.tensor_reduce(
+            out=mask[:],
+            in_=ident[:].rearrange("p (r q h) -> p q r h", q=Q, h=H),
+            axis=mybir.AxisListType.XY,
+            op=ADD,
+        )
+        nc.vector.tensor_copy(
+            out=perm[:].rearrange("p (r q) -> p r q", q=Q), in_=ident[:].rearrange("p (q r) -> p r q", q=Q)
+        )
 
         scl = keep.tile([P, D], F32, name="scl")
         for b in range(2):
@@ -99,29 +113,42 @@ def tile_productkeysoftmemoryplus_w4_kernel(
             else:
                 nc.vector.tensor_copy(out=scl[:, 512:1024], in_=ps[:])
 
-        S = {}
-
-        def xs(s, q):
+        def xs(n):
             t = work.tile([P, D], BF16, name="xs", align_bytes=64)
-            nc.vector.tensor_tensor(out=t[:], in0=xb[s][:, q, :].bitcast(FP8), in1=scl[:], op=MUL)
-            S["xs", s, q] = t
+            src, k = X_AT[n]
+            nc.vector.tensor_tensor(out=t[:], in0=src[:, k, :].bitcast(FP8), in1=scl[:], op=MUL)
+            S["xs", n] = t
 
-        def xt(s, q):
-            xw = S["xs", s, q][:].bitcast(F32)
+        def xt(n):
+            xw = S["xs", n][:].bitcast(F32)
             ps = pst.tile([P, PASSES, 2, P], F32, name="tp")
             for g in range(PASSES):
                 for u in range(2):
                     nc.tensor.transpose(ps[:, g, u, :], xw[:, 256 * g + u : 256 * (g + 1) : 2], ident[:])
-            xg = work.tile([P, PASSES, P, PACK], BF16, name="xg", align_bytes=64)
-            nc.scalar.copy(
-                out=xg[:].rearrange("p g r t -> p (g r t)").bitcast(F32).rearrange("p (g r u) -> p g r u", g=PASSES, u=2),
-                in_=ps[:].rearrange("p g u r -> p g r u"),
+            S["xt", n] = ps
+
+        def copy_out(eng, dst, src):
+            if eng == "V":
+                nc.vector.tensor_copy(out=dst, in_=src)
+            else:
+                nc.scalar.copy(out=dst, in_=src)
+
+        def interleave(eng, ps):
+            t = work.tile([P, PASSES, P, PACK], BF16, name="xg", align_bytes=64)
+            copy_out(
+                eng,
+                t[:].rearrange("p g r t -> p (g r t)").bitcast(F32).rearrange("p (g r u) -> p g r u", g=PASSES, u=2),
+                ps[:].rearrange("p g u r -> p g r u"),
             )
-            S["xg", s, q] = xg
+            return t
+
+        def xc(n, eng="S"):
+            S["xg", n] = interleave(eng, S["xt", n])
 
         def quant(src, key):
-            c = keep.tile([P, PASSES, P], U32, name="c_" + "_".join(str(k) for k in key), align_bytes=64)
-            sc = keep.tile([P, PASSES, P], U8, name="s_" + "_".join(str(k) for k in key), align_bytes=64)
+            nm = key[0] + str(key[1])
+            c = keep.tile([P, PASSES, P], U32, name="c_" + nm, align_bytes=64)
+            sc = keep.tile([P, PASSES, P], U8, name="s_" + nm, align_bytes=64)
             nc.vector.quantize_mx(
                 out=c[:].rearrange("p g r -> p (g r)").bitcast(E4M3X4),
                 scales=sc[:].rearrange("p g r -> p (g r)"),
@@ -129,10 +156,10 @@ def tile_productkeysoftmemoryplus_w4_kernel(
             )
             S[key] = (c, sc)
 
-        def qx(s, q):
-            quant(S["xg", s, q], ("x", s, q))
+        def qx(n):
+            quant(S["xg", n], ("x", n))
 
-        def mx(ps, key, w, wsc, n0, n):
+        def mm(ps, key, w, wsc, n0, n):
             codes, scales = S[key]
             for g in range(PASSES):
                 nc.tensor.matmul_mx(
@@ -145,199 +172,437 @@ def tile_productkeysoftmemoryplus_w4_kernel(
                     stop=(g == PASSES - 1),
                 )
 
-        for s in range(HALVES):
-            S["e", s] = keep.tile([P, H, Q, 2, N], F32, name=f"e{s}")
-            S["z", s] = keep.tile([P, H, Q, 2], F32, name=f"z{s}")
+        for n in range(NT):
+            S["e", n] = keep.tile([P, H, 2, N], F32, name=f"e{n}")
+            S["z", n] = keep.tile([P, H, 2], F32, name=f"z{n}")
+            S["top", n] = keep.tile([P, H, 2], F32, name=f"top{n}")
+            S["rz", n] = keep.tile([P, H], F32, name=f"rz{n}")
 
-        def sc(s, k):
-            ps = psm.tile([P, 2, C], F32, name="mm")
-            for m in range(2):
-                for n0 in (0, 128):
-                    mx(ps[:, m, n0 : n0 + 128], ("x", s, 2 * k + m), wk_w, wk_s, n0, 128)
-            S["sc", s, k] = ps
+        def sc(n):
+            ps = psm.tile([P, C], F32, name="mm")
+            for n0 in (0, 128):
+                mm(ps[:, n0 : n0 + 128], ("x", n), wk_w, wk_s, n0, 128)
+            S["sc", n] = ps
 
-        def mxs(s, k):
-            ps = S["sc", s, k]
-            top = work.tile([P, 2, H, 2], F32, name="top")
+        def mx(n):
             nc.vector.tensor_reduce(
-                out=top[:].rearrange("p k h a -> p (k h a)"),
-                in_=ps[:].rearrange("p k (h a n) -> p (k h a) n", h=H, a=2),
+                out=S["top", n][:].rearrange("p h a -> p (h a)"),
+                in_=S["sc", n][:].rearrange("p (c n) -> p c n", n=N),
                 axis=AX,
                 op=MAX,
             )
-            S["top", s, k] = top
 
-        def sub(s, q):
-            e = S["e", s]
-            nc.vector.tensor_tensor(
-                out=e[:, :, q, :, :],
-                in0=S["sc", s, q // 2][:, q % 2, :].rearrange("p (h a n) -> p h a n", h=H, a=2),
-                in1=S["top", s, q // 2][:, q % 2, :, :].unsqueeze(3).to_broadcast([P, H, 2, N]),
-                op=SUB,
+        def neg(n):
+            nc.vector.tensor_scalar(out=S["top", n][:], in0=S["top", n][:], scalar1=-1.0, scalar2=None, op0=MUL)
+
+        def ex(n):
+            ps, e, top, z = S["sc", n], S["e", n], S["top", n], S["z", n]
+            for h in range(H):
+                for a in range(2):
+                    k = 2 * h + a
+                    nc.scalar.activation(
+                        out=e[:, h, a, :],
+                        in_=ps[:, N * k : N * k + N],
+                        func=EXP,
+                        bias=top[:, h, a : a + 1],
+                        accum_out=z[:, h, a : a + 1],
+                    )
+
+        def nz(n):
+            z = S["z", n]
+            nc.vector.tensor_tensor(out=S["rz", n][:], in0=z[:, :, 0], in1=z[:, :, 1], op=MUL)
+
+        def nr(n):
+            nc.vector.reciprocal(out=S["rz", n][:], in_=S["rz", n][:])
+
+        def norm(n):
+            first = S["e", n][:, :, 0, :]
+            nc.vector.tensor_tensor(out=first, in0=first, in1=S["rz", n][:].unsqueeze(2).to_broadcast([P, H, N]), op=MUL)
+
+        def park_rows(n, k):
+            return out[768 + 32 * n : 768 + 32 * (n + k), :]
+
+        def park(n):
+            nc.sync.dma_start(
+                out=park_rows(n, 1).rearrange("r (q f) -> (r q) f", q=Q), in_=S["e", n][:].rearrange("p h a n -> p (h a n)")
             )
-            nc.scalar.activation(out=e[:, :, q, :, :], in_=e[:, :, q, :, :], func=EXP)
 
-        def sm(s, q):
-            nc.vector.tensor_reduce(out=S["z", s][:, :, q, :], in_=S["e", s][:, :, q, :, :], axis=AX, op=ADD)
+        def ld(c):
+            rows = park_rows(BATCHES[c][0], len(BATCHES[c])).rearrange("(g r) (c a n) -> a (r c) g n", r=8, a=2, n=N)
+            nc.sync.dma_start(out=left_c[c][:], in_=rows[0])
 
-        def norm(s):
-            e, z = S["e", s], S["z", s]
-            zz = work.tile([P, H, Q], F32, name="zz")
-            nc.vector.tensor_tensor(out=zz[:], in0=z[:, :, :, 0], in1=z[:, :, :, 1], op=MUL)
-            rz = work.tile([P, H, Q], F32, name="rz")
-            nc.vector.reciprocal(out=rz[:], in_=zz[:])
-            first = e[:, :, :, 0, :].rearrange("p h q n -> p (h q) n")
-            nc.vector.tensor_tensor(
-                out=first, in0=first, in1=rz[:].rearrange("p h q -> p (h q)").unsqueeze(2).to_broadcast([P, H * Q, N]), op=MUL
-            )
-            park = out[768 + 128 * s : 896 + 128 * s, :]
-            nc.sync.dma_start(out=park, in_=e[:].rearrange("p h q a n -> p (h q a n)"))
-            for r in range(8):
-                src = park.rearrange("(g r) (c a n) -> r c g a n", r=8, a=2, n=N)[r][:, :, 1, :]
-                nc.sync.dma_start(out=right[s][16 * r : 16 * r + 16, :, r, :], in_=src)
-            for q in range(Q):
-                src = park.rearrange("(g r) (h q a n) -> r h g q a n", r=8, h=H, q=Q, a=2)[:, :, :, q, 0, :]
-                nc.sync.dma_start(out=left[s][q : P : Q, :, q, :], in_=src.rearrange("r h g n -> (r h) g n"))
+        def rd(c, r):
+            rows = park_rows(BATCHES[c][0], len(BATCHES[c])).rearrange("(g r) (c a n) -> a (r c) g n", r=8, a=2, n=N)
+            nc.sync.dma_start(out=right[c][16 * r : 16 * r + 16, :, r, :], in_=rows[1][16 * r : 16 * r + 16])
 
-        def gate(s, q, b):
-            if b == 0:
-                S["gate", s, q] = keep.tile([P, D], F32, name=f"gate{s}{q}")
+        def lm(c, q, eng="V"):
+            if eng == "V":
+                nc.vector.tensor_scalar(out=left[c][:, :, q, :], in0=left_c[c][:], scalar1=mask[:, q : q + 1], scalar2=None, op0=MUL)
+            elif eng == "G":
+                nc.gpsimd.tensor_scalar(
+                    out=left[c][:, :, q, :], in0=left_c[c][:], scalar1=mask[:, q : q + 1], scalar2=0.0, op0=MUL, op1=ADD
+                )
+            else:
+                nc.scalar.activation(out=left[c][:, :, q, :], in_=left_c[c][:], func=COPY, scale=mask[:, q : q + 1])
+
+        def gate(n, b):
+            if ("gate", n) not in S:
+                S["gate", n] = keep.tile([P, D], F32, name=f"gate{n}")
             ps = psm.tile([P, 512], F32, name="mm")
-            mx(ps[:], ("x", s, q), wg_w, wg_s, 512 * b, 512)
-            nc.scalar.activation(out=S["gate", s, q][:, 512 * b : 512 * b + 512], in_=ps[:], func=SILU)
+            mm(ps[:], ("x", n), wg_w, wg_s, 512 * b, 512)
+            S["a", n, b] = ps
 
-        for s in range(HALVES):
-            S["wt", s] = keep.tile([P, 16, P, 2], BF16, name=f"wt{s}", align_bytes=64)
-            S["u1", s] = keep.tile([P, 2, Q, N, 8], F32, name=f"u1{s}")
+        def silu(n, b):
+            nc.scalar.activation(out=S["gate", n][:, 512 * b : 512 * b + 512], in_=S["a", n, b][:], func=SILU)
 
-        def prod(s, b):
+        for n in range(NT):
+            S["wt", n] = keep.tile([P, 16, 32, 2], BF16, name=f"wt{n}", align_bytes=64)
+            S["u1", n] = keep.tile([P, 2, 32, 8], F32, name=f"u1{n}", align_bytes=64)
+
+        def prod(n, b):
             ps = psm.tile([P, 2, 8 * N], F32, name="mm")
+            c, g0 = place[n]
             for k in range(2):
-                grp = 2 * b + k
+                grp = g0 + 2 * b + k
                 nc.tensor.matmul(
                     out=ps[:, k, :],
-                    lhsT=left[s][:, grp, :, :].rearrange("p q n -> p (q n)"),
-                    rhs=right[s][:, grp, :, :].rearrange("p r n -> p (r n)"),
+                    lhsT=left[c][:, grp, :, :].rearrange("p q n -> p (q n)"),
+                    rhs=right[c][:, grp, :, :].rearrange("p r n -> p (r n)"),
                     start=True,
                     stop=True,
                 )
-            S["pr", s, b] = ps
+            S["pr", n, b] = ps
 
-        def gn(s, b):
+        def gn(n, b):
             nc.vector.tensor_tensor(
-                out=S["wt", s][:, :, 16 * b : 16 * b + 16, :],
-                in0=S["pr", s, b][:].rearrange("p k (r w e) -> p w (k r) e", r=8, e=2),
+                out=S["wt", n][:, :, 16 * b : 16 * b + 16, :],
+                in0=S["pr", n, b][:].rearrange("p k (r w e) -> p w (k r) e", r=8, e=2),
                 in1=gain[:].rearrange("p (w e) -> p w e", e=2).unsqueeze(2).to_broadcast([P, 16, 16, 2]),
                 op=MUL,
             )
 
-        def t1(s, b, vec=False):
-            words = S["wt", s][:].rearrange("p w r e -> p (w r e)").bitcast(F32)
-            u, jh = b // 2, b % 2
-            ps = pst.tile([P, 4, P], F32, name="tp")
-            for c in range(4):
-                w = 2 * (4 * jh + c) + u
-                nc.tensor.transpose(ps[:, c, :], words[:, 128 * w : 128 * w + 128], ident[:])
-            dst = S["u1", s][:, u, :, :, 4 * jh : 4 * jh + 4].rearrange("p q i c -> p (q i) c")
-            src = ps[:].rearrange("p c m -> p m c")
-            if vec:
-                nc.vector.tensor_copy(out=dst, in_=src)
-            else:
-                nc.scalar.copy(out=dst, in_=src)
+        def vt(n):
+            S["ut", n] = work.tile([P, 16, 32], F32, name="ut", align_bytes=64)
+            nc.vector.transpose(
+                out=S["ut", n][:].rearrange("p w i -> p (w i)"),
+                in_=S["wt", n][:].rearrange("p w r e -> p (w r e)").bitcast(F32),
+            )
 
-        def t2(s, q):
+        def t1c(n, eng="S"):
+            src = S["ut", n][:].rearrange("p (a c u) i -> p u a i c", a=2, u=2)
+            dst = S["u1", n][:].rearrange("p u i (a c) -> p u a i c", a=2)
+            for u in range(2):
+                copy_out(eng, dst[:, u], src[:, u])
+
+        def t2(n):
             ps = pst.tile([P, PASSES, 2, P], F32, name="tp")
             for g in range(PASSES):
                 for u in range(2):
                     nc.tensor.transpose(
-                        ps[:, g, u, :], S["u1", s][:, u, q, 16 * g : 16 * g + 16, :].rearrange("p i j -> p (i j)"), ident[:]
+                        ps[:, g, u, :], S["u1", n][:, u, 16 * g : 16 * g + 16, :].rearrange("p i j -> p (i j)"), perm[:]
                     )
-            ug = work.tile([P, PASSES, P, PACK], BF16, name="xg", align_bytes=64)
-            nc.scalar.copy(
-                out=ug[:].rearrange("p g r t -> p (g r t)").bitcast(F32).rearrange("p (g r u) -> p g r u", g=PASSES, u=2),
-                in_=ps[:].rearrange("p g u r -> p g r u"),
-            )
-            S["ug", s, q] = ug
+            S["t2", n] = ps
 
-        def qu(s, q):
-            quant(S["ug", s, q], ("u", s, q))
+        def t2c(n, eng="S"):
+            S["ug", n] = interleave(eng, S["t2", n])
 
-        def val(s, q, b):
+        def qu(n):
+            quant(S["ug", n], ("u", n))
+
+        def val(n, b):
             ps = psm.tile([P, 512], F32, name="mm")
-            mx(ps[:], ("u", s, q), v_w, v_s, 512 * b, 512)
-            S["mem", s, q, b] = ps
+            mm(ps[:], ("u", n), v_w, v_s, 512 * b, 512)
+            S["mem", n, b] = ps
 
-        def fin(s, q, b):
-            if b == 0:
-                S["res", s, q] = work.tile([P, D], F32, name="res")
+        def fin(n, b):
+            g = S["gate", n][:, 512 * b : 512 * b + 512]
+            nc.vector.tensor_tensor(out=g, in0=S["mem", n, b][:], in1=g, op=MUL)
+
+        def st(n):
+            nc.sync.dma_start(out=out[128 * n : 128 * n + 128, :], in_=S["gate", n][:])
+
+        def sth(n, b):
             sl = slice(512 * b, 512 * b + 512)
-            nc.vector.tensor_tensor(out=S["res", s, q][:, sl], in0=S["mem", s, q, b][:], in1=S["gate", s, q][:, sl], op=MUL)
-            if b == 1:
-                nc.sync.dma_start(out=out_view[s][:, q, :], in_=S["res", s, q][:])
+            nc.sync.dma_start(out=out[128 * n : 128 * n + 128, sl], in_=S["gate", n][:, sl])
 
-        A, B = 0, 1
-        xs(A, 0); xt(A, 0)
-        xs(A, 1); xt(A, 1)
-        xs(A, 2); qx(A, 0); xt(A, 2)
-        xs(A, 3); qx(A, 1); xt(A, 3)
-        sc(A, 0)
-        qx(A, 2)
-        mxs(A, 0); sub(A, 0); sub(A, 1)
-        qx(A, 3)
-        sc(A, 1)
-        sm(A, 0); mxs(A, 1); sub(A, 2); sm(A, 1); sub(A, 3)
-        xs(B, 0)
-        sm(A, 2); sm(A, 3)
-        norm(A)
-        gate(A, 0, 0); gate(A, 0, 1)
-        xt(B, 0)
-        xs(B, 1); gate(A, 1, 0); gate(A, 1, 1); xt(B, 1)
-        qx(B, 0)
-        xs(B, 2); gate(A, 2, 0); gate(A, 2, 1); xt(B, 2)
-        qx(B, 1)
-        sc(B, 0)
-        xs(B, 3); gate(A, 3, 0); gate(A, 3, 1); xt(B, 3)
-        qx(B, 2)
-        mxs(B, 0); sub(B, 0); sub(B, 1)
-        qx(B, 3)
-        sc(B, 1)
-        prod(A, 0); sm(B, 0); mxs(B, 1); sub(B, 2); sm(B, 1); sub(B, 3)
-        gn(A, 0)
-        prod(A, 1); sm(B, 2); sm(B, 3); norm(B); gn(A, 1)
-        for b in range(2, 8):
-            prod(A, b); gn(A, b)
-        gate(B, 0, 0); gate(B, 0, 1)
-        for b in range(4):
-            t1(A, b)
-        gate(B, 1, 0); gate(B, 1, 1)
-        prod(B, 0); gn(B, 0)
-        gate(B, 2, 0); gate(B, 2, 1)
-        t2(A, 0)
-        prod(B, 1); gn(B, 1); qu(A, 0)
-        val(A, 0, 0); val(A, 0, 1)
-        prod(B, 2); gn(B, 2); fin(A, 0, 0); fin(A, 0, 1)
-        t2(A, 1)
-        gate(B, 3, 0); gate(B, 3, 1)
-        prod(B, 3); gn(B, 3); qu(A, 1)
-        val(A, 1, 0); val(A, 1, 1)
-        prod(B, 4); gn(B, 4); fin(A, 1, 0); fin(A, 1, 1)
-        t2(A, 2)
-        prod(B, 5); gn(B, 5); qu(A, 2)
-        prod(B, 6); gn(B, 6)
-        prod(B, 7); gn(B, 7)
-        val(A, 2, 0); val(A, 2, 1)
-        t2(A, 3)
-        t1(B, 0); t1(B, 1, True)
-        qu(A, 3); fin(A, 2, 0); fin(A, 2, 1)
-        t1(B, 2); t1(B, 3, True)
-        val(A, 3, 0); val(A, 3, 1)
-        t2(B, 0); qu(B, 0)
-        t2(B, 1); fin(A, 3, 0); fin(A, 3, 1); qu(B, 1)
-        val(B, 0, 0); val(B, 0, 1)
-        t2(B, 2); fin(B, 0, 0); qu(B, 2); fin(B, 0, 1)
-        val(B, 1, 0); val(B, 1, 1)
-        t2(B, 3); fin(B, 1, 0); qu(B, 3); fin(B, 1, 1)
-        val(B, 2, 0); val(B, 2, 1)
-        fin(B, 2, 0); fin(B, 2, 1)
-        val(B, 3, 0); val(B, 3, 1)
-        fin(B, 3, 0); fin(B, 3, 1)
+        xs(1)
+        xs(0)
+        xt(1)
+        xc(1)
+        xs(3)
+        xt(0)
+        xt(3)
+        qx(1)
+        xs(4)
+        sc(1)
+        xc(0)
+        mx(1)
+        xc(3)
+        xt(4)
+        qx(0)
+        neg(1)
+        xs(2)
+        sc(0)
+        ex(1)
+        xt(2)
+        mx(0)
+        xc(4)
+        nz(1)
+        neg(0)
+        xs(5)
+        ex(0)
+        nr(1)
+        qx(4)
+        nz(0)
+        norm(1)
+        xt(5)
+        sc(4)
+        qx(3)
+        nr(0)
+        xc(2)
+        qx(2)
+        park(1)
+        norm(0)
+        mx(4)
+        neg(4)
+        sc(3)
+        xc(5)
+        mx(3)
+        ex(4)
+        park(0)
+        sc(2)
+        rd(0, 5)
+        mx(2)
+        qx(5)
+        sc(5)
+        neg(2)
+        gate(1, 1)
+        neg(3)
+        rd(0, 6)
+        xs(7)
+        ex(2)
+        rd(0, 2)
+        mx(5)
+        ex(3)
+        nz(2)
+        neg(5)
+        xs(6)
+        rd(0, 7)
+        gate(2, 1)
+        nr(2)
+        gate(1, 0)
+        rd(0, 3)
+        xt(7)
+        rd(0, 1)
+        xt(6)
+        gate(0, 0)
+        nz(3)
+        ex(5)
+        nz(5)
+        rd(0, 4)
+        nz(4)
+        ld(0)
+        gate(0, 1)
+        gate(5, 0)
+        nr(3)
+        nr(5)
+        xc(7, "V")
+        rd(0, 0)
+        silu(1, 1)
+        nr(4)
+        silu(2, 1)
+        norm(2)
+        norm(3)
+        lm(0, 3)
+        silu(1, 0)
+        silu(0, 0)
+        qx(7)
+        park(3)
+        gate(7, 0)
+        norm(4)
+        lm(0, 1)
+        park(4)
+        gate(5, 1)
+        park(2)
+        lm(0, 2)
+        silu(0, 1)
+        xc(6, "V")
+        lm(0, 0)
+        silu(5, 0)
+        rd(1, 2)
+        prod(0, 1)
+        qx(6)
+        sc(7)
+        mx(7)
+        prod(0, 0)
+        norm(5)
+        gn(0, 1)
+        silu(5, 1)
+        neg(7)
+        gn(0, 0)
+        rd(1, 3)
+        prod(1, 1)
+        vt(0)
+        ld(1)
+        silu(7, 0)
+        sc(6)
+        ex(7)
+        mx(6)
+        neg(6)
+        prod(1, 0)
+        rd(1, 1)
+        ex(6)
+        gn(1, 1)
+        gate(4, 0)
+        park(5)
+        rd(1, 5)
+        nz(7)
+        gate(2, 0)
+        lm(1, 3, "S")
+        lm(1, 1)
+        lm(1, 0)
+        rd(1, 4)
+        gate(3, 1)
+        rd(1, 7)
+        lm(1, 2, "S")
+        gn(1, 0)
+        rd(1, 6)
+        nr(7)
+        nz(6)
+        gate(3, 0)
+        rd(1, 0)
+        norm(7)
+        nr(6)
+        prod(4, 0)
+        t1c(0, "V")
+        silu(4, 0)
+        t2(0)
+        norm(6)
+        prod(3, 0)
+        vt(1)
+        t1c(1, "V")
+        gn(4, 0)
+        park(7)
+        t2c(0, "V")
+        silu(2, 0)
+        t2(1)
+        qu(0)
+        t2c(1)
+        prod(4, 1)
+        park(6)
+        gn(3, 0)
+        rd(2, 2)
+        qu(1)
+        rd(2, 3)
+        rd(2, 5)
+        gn(4, 1)
+        val(0, 0)
+        ld(2)
+        rd(2, 7)
+        silu(3, 1)
+        silu(3, 0)
+        fin(0, 0)
+        val(0, 1)
+        prod(3, 1)
+        rd(2, 0)
+        rd(2, 1)
+        rd(2, 4)
+        fin(0, 1)
+        st(0)
+        vt(4)
+        lm(2, 0)
+        lm(2, 2, "S")
+        gn(3, 1)
+        prod(2, 0)
+        prod(2, 1)
+        rd(2, 6)
+        vt(3)
+        lm(2, 3)
+        lm(2, 1, "S")
+        val(1, 0)
+        gn(2, 0)
+        prod(5, 0)
+        t1c(3, "V")
+        gn(2, 1)
+        fin(1, 0)
+        prod(5, 1)
+        t1c(4)
+        t2(4)
+        gn(5, 0)
+        prod(6, 1)
+        gn(5, 1)
+        t2c(4)
+        vt(2)
+        vt(5)
+        gn(6, 1)
+        t2(3)
+        prod(6, 0)
+        prod(7, 0)
+        t2c(3, "V")
+        t1c(5)
+        t1c(2)
+        gn(6, 0)
+        qu(4)
+        t2(5)
+        vt(6)
+        t2(2)
+        prod(7, 1)
+        gn(7, 0)
+        t2c(5)
+        val(1, 1)
+        t1c(6)
+        gate(4, 1)
+        qu(3)
+        val(4, 1)
+        t2c(2)
+        val(4, 0)
+        qu(5)
+        gn(7, 1)
+        fin(1, 1)
+        st(1)
+        val(3, 1)
+        silu(4, 1)
+        qu(2)
+        vt(7)
+        fin(4, 1)
+        val(3, 0)
+        val(2, 1)
+        t1c(7)
+        fin(4, 0)
+        st(4)
+        fin(3, 1)
+        fin(3, 0)
+        st(3)
+        val(2, 0)
+        t2(7)
+        t2(6)
+        t2c(7)
+        fin(2, 1)
+        val(5, 1)
+        val(5, 0)
+        fin(2, 0)
+        st(2)
+        qu(7)
+        t2c(6)
+        gate(6, 0)
+        gate(7, 1)
+        silu(7, 1)
+        fin(5, 1)
+        fin(5, 0)
+        st(5)
+        val(7, 0)
+        qu(6)
+        fin(7, 0)
+        sth(7, 0)
+        val(7, 1)
+        silu(6, 0)
+        gate(6, 1)
+        fin(7, 1)
+        sth(7, 1)
+        silu(6, 1)
+        val(6, 0)
+        val(6, 1)
+        fin(6, 0)
+        sth(6, 0)
+        fin(6, 1)
+        sth(6, 1)

@@ -88,18 +88,9 @@ def tile_productkeysoftmemoryplus_w4_kernel(
             left.append(keep.tile([P, 4 * len(tiles), Q, N], F32, name=f"left{c}"))
             left_c.append(keep.tile([P, 4 * len(tiles), N], F32, name=f"left_c{c}"))
             right.append(keep.tile([P, 4 * len(tiles), 8, N], F32, name=f"right{c}"))
-            nc.gpsimd.memset(right[c][:], 0.0)
+            (nc.gpsimd if c == 2 else nc.vector).memset(right[c][:], 0.0)
         for q in range(Q):
-            nc.gpsimd.dma_start(out=gain[32 * q : 32 * q + 32, :], in_=slot_gain.rearrange("(i j) -> i j", j=N))
-        nc.vector.tensor_reduce(
-            out=mask[:],
-            in_=ident[:].rearrange("p (r q h) -> p q r h", q=Q, h=H),
-            axis=mybir.AxisListType.XY,
-            op=ADD,
-        )
-        nc.vector.tensor_copy(
-            out=perm[:].rearrange("p (r q) -> p r q", q=Q), in_=ident[:].rearrange("p (q r) -> p r q", q=Q)
-        )
+            nc.sync.dma_start(out=gain[32 * q : 32 * q + 32, :], in_=slot_gain.rearrange("(i j) -> i j", j=N))
 
         scl = keep.tile([P, D], F32, name="scl")
         for b in range(2):
@@ -112,6 +103,17 @@ def tile_productkeysoftmemoryplus_w4_kernel(
                 nc.scalar.copy(out=scl[:, 0:512], in_=ps[:])
             else:
                 nc.vector.tensor_copy(out=scl[:, 512:1024], in_=ps[:])
+
+        def consts():
+            nc.vector.tensor_reduce(
+                out=mask[:],
+                in_=ident[:].rearrange("p (r q h) -> p q r h", q=Q, h=H),
+                axis=mybir.AxisListType.XY,
+                op=ADD,
+            )
+            nc.vector.tensor_copy(
+                out=perm[:].rearrange("p (r q) -> p r q", q=Q), in_=ident[:].rearrange("p (q r) -> p r q", q=Q)
+            )
 
         def xs(n):
             t = work.tile([P, D], BF16, name="xs", align_bytes=64)
@@ -330,279 +332,280 @@ def tile_productkeysoftmemoryplus_w4_kernel(
         xt(1)
         xc(1)
         xs(3)
-        xt(0)
-        xt(3)
         qx(1)
-        xs(4)
-        sc(1)
+        xt(0)
         xc(0)
-        mx(1)
-        xc(3)
-        xt(4)
-        qx(0)
-        neg(1)
         xs(2)
+        qx(0)
+        sc(1)
+        xt(3)
         sc(0)
-        ex(1)
+        xc(3)
+        mx(1)
+        xs(4)
+        qx(3)
         xt(2)
+        xc(2)
+        xt(4)
         mx(0)
-        xc(4)
-        nz(1)
-        neg(0)
+        neg(1)
         xs(5)
+        neg(0)
+        ex(1)
+        sc(3)
+        xc(4, "V")
+        qx(2)
+        consts()
+        nz(1)
+        mx(3)
         ex(0)
         nr(1)
+        xt(5)
         qx(4)
         nz(0)
-        norm(1)
-        xt(5)
-        sc(4)
-        qx(3)
-        nr(0)
-        xc(2)
-        qx(2)
-        park(1)
-        norm(0)
-        mx(4)
-        neg(4)
-        sc(3)
-        xc(5)
-        mx(3)
-        ex(4)
-        park(0)
-        sc(2)
-        rd(0, 5)
-        mx(2)
-        qx(5)
-        sc(5)
-        neg(2)
-        gate(1, 1)
         neg(3)
-        rd(0, 6)
-        xs(7)
-        ex(2)
-        rd(0, 2)
-        mx(5)
+        sc(2)
+        norm(1)
+        nr(0)
+        xc(5)
+        sc(4)
+        mx(2)
+        norm(0)
+        park(1)
+        park(0)
+        rd(0, 5)
+        neg(2)
+        qx(5)
         ex(3)
-        nz(2)
-        neg(5)
-        xs(6)
-        rd(0, 7)
+        mx(4)
+        sc(5)
+        neg(4)
+        ex(2)
         gate(2, 1)
-        nr(2)
-        gate(1, 0)
-        rd(0, 3)
-        xt(7)
-        rd(0, 1)
-        xt(6)
-        gate(0, 0)
+        gate(5, 1)
+        mx(5)
+        nz(2)
         nz(3)
-        ex(5)
-        nz(5)
-        rd(0, 4)
-        nz(4)
         ld(0)
+        neg(5)
         gate(0, 1)
         gate(5, 0)
-        nr(3)
+        xs(7)
+        ex(4)
+        nz(4)
+        rd(0, 4)
+        nr(2)
+        xt(7)
+        xs(6)
+        ex(5)
+        nz(5)
         nr(5)
-        xc(7, "V")
-        rd(0, 0)
-        silu(1, 1)
-        nr(4)
-        silu(2, 1)
+        rd(0, 3)
         norm(2)
-        norm(3)
-        lm(0, 3)
-        silu(1, 0)
-        silu(0, 0)
-        qx(7)
-        park(3)
-        gate(7, 0)
-        norm(4)
-        lm(0, 1)
-        park(4)
-        gate(5, 1)
-        park(2)
-        lm(0, 2)
-        silu(0, 1)
-        xc(6, "V")
-        lm(0, 0)
-        silu(5, 0)
-        rd(1, 2)
-        prod(0, 1)
-        qx(6)
-        sc(7)
-        mx(7)
-        prod(0, 0)
-        norm(5)
-        gn(0, 1)
+        silu(2, 1)
+        gate(1, 0)
+        rd(0, 1)
         silu(5, 1)
-        neg(7)
-        gn(0, 0)
-        rd(1, 3)
-        prod(1, 1)
-        vt(0)
-        ld(1)
+        nr(4)
+        gate(0, 0)
+        xc(7, "V")
+        silu(0, 1)
+        xt(6)
+        rd(0, 0)
+        norm(5)
+        norm(4)
+        silu(1, 0)
+        nr(3)
+        lm(0, 1)
+        gate(1, 1)
+        silu(5, 0)
+        norm(3)
+        rd(0, 7)
+        rd(0, 6)
+        rd(0, 2)
+        qx(7)
+        park(2)
+        park(4)
+        gate(7, 0)
         silu(7, 0)
+        sc(7)
+        xc(6, "V")
+        lm(0, 3)
+        qx(6)
         sc(6)
-        ex(7)
+        lm(0, 0)
+        park(3)
+        lm(0, 2)
+        ld(1)
+        rd(1, 5)
+        prod(1, 1)
+        rd(1, 3)
+        rd(1, 2)
+        rd(1, 4)
+        silu(0, 0)
+        mx(7)
         mx(6)
         neg(6)
-        prod(1, 0)
-        rd(1, 1)
+        silu(1, 1)
+        neg(7)
+        ex(7)
         ex(6)
+        prod(0, 0)
+        rd(1, 1)
         gn(1, 1)
-        gate(4, 0)
-        park(5)
-        rd(1, 5)
+        gn(0, 0)
         nz(7)
-        gate(2, 0)
-        lm(1, 3, "S")
-        lm(1, 1)
-        lm(1, 0)
-        rd(1, 4)
-        gate(3, 1)
-        rd(1, 7)
-        lm(1, 2, "S")
+        park(5)
+        lm(1, 0, "S")
+        prod(1, 0)
         gn(1, 0)
+        prod(0, 1)
+        lm(1, 2, "S")
+        gate(2, 0)
         rd(1, 6)
-        nr(7)
-        nz(6)
         gate(3, 0)
+        nr(7)
+        lm(1, 1, "S")
+        nz(6)
+        nr(6)
+        gn(0, 1)
+        silu(2, 0)
+        lm(1, 3)
+        rd(1, 7)
+        norm(6)
         rd(1, 0)
         norm(7)
-        nr(6)
-        prod(4, 0)
-        t1c(0, "V")
-        silu(4, 0)
-        t2(0)
-        norm(6)
-        prod(3, 0)
-        vt(1)
-        t1c(1, "V")
-        gn(4, 0)
         park(7)
-        t2c(0, "V")
-        silu(2, 0)
-        t2(1)
-        qu(0)
-        t2c(1)
-        prod(4, 1)
-        park(6)
-        gn(3, 0)
-        rd(2, 2)
-        qu(1)
-        rd(2, 3)
-        rd(2, 5)
-        gn(4, 1)
-        val(0, 0)
-        ld(2)
-        rd(2, 7)
-        silu(3, 1)
-        silu(3, 0)
-        fin(0, 0)
-        val(0, 1)
-        prod(3, 1)
-        rd(2, 0)
-        rd(2, 1)
-        rd(2, 4)
-        fin(0, 1)
-        st(0)
-        vt(4)
-        lm(2, 0)
-        lm(2, 2, "S")
-        gn(3, 1)
+        vt(0)
+        t1c(0, "V")
+        gate(3, 1)
+        vt(1)
+        gate(4, 0)
         prod(2, 0)
         prod(2, 1)
-        rd(2, 6)
-        vt(3)
-        lm(2, 3)
-        lm(2, 1, "S")
-        val(1, 0)
+        silu(4, 0)
         gn(2, 0)
-        prod(5, 0)
-        t1c(3, "V")
+        t2(0)
+        park(6)
+        t1c(1)
+        t2c(0, "V")
+        silu(3, 0)
+        prod(4, 0)
+        qu(0)
+        t2(1)
+        rd(2, 2)
+        silu(3, 1)
+        rd(2, 4)
+        gn(4, 0)
+        ld(2)
+        t2c(1)
+        prod(4, 1)
+        val(0, 1)
+        lm(2, 1, "S")
+        val(0, 0)
+        rd(2, 6)
         gn(2, 1)
+        qu(1)
+        gn(4, 1)
+        lm(2, 2, "S")
+        rd(2, 1)
+        rd(2, 7)
+        fin(0, 1)
+        val(1, 1)
+        fin(0, 0)
+        st(0)
+        val(1, 0)
+        rd(2, 3)
+        rd(2, 5)
+        fin(1, 1)
         fin(1, 0)
+        st(1)
+        lm(2, 0, "S")
+        prod(3, 1)
+        lm(2, 3, "S")
+        rd(2, 0)
+        prod(3, 0)
+        vt(4)
+        vt(2)
+        gn(3, 1)
+        t1c(2)
+        gn(3, 0)
+        prod(5, 0)
         prod(5, 1)
+        t2(2)
+        vt(3)
         t1c(4)
-        t2(4)
+        t1c(3, "V")
         gn(5, 0)
+        t2(4)
+        t2c(2)
         prod(6, 1)
         gn(5, 1)
-        t2c(4)
-        vt(2)
+        prod(6, 0)
+        qu(2)
+        t2(3)
         vt(5)
         gn(6, 1)
-        t2(3)
-        prod(6, 0)
-        prod(7, 0)
-        t2c(3, "V")
+        t2c(4)
         t1c(5)
-        t1c(2)
         gn(6, 0)
-        qu(4)
+        prod(7, 0)
         t2(5)
-        vt(6)
-        t2(2)
         prod(7, 1)
-        gn(7, 0)
-        t2c(5)
-        val(1, 1)
-        t1c(6)
-        gate(4, 1)
-        qu(3)
-        val(4, 1)
-        t2c(2)
+        qu(4)
+        vt(6)
         val(4, 0)
-        qu(5)
+        gn(7, 0)
+        t2c(3)
+        qu(3)
+        gate(4, 1)
+        val(4, 1)
         gn(7, 1)
-        fin(1, 1)
-        st(1)
-        val(3, 1)
         silu(4, 1)
-        qu(2)
-        vt(7)
-        fin(4, 1)
-        val(3, 0)
-        val(2, 1)
-        t1c(7)
         fin(4, 0)
-        st(4)
-        fin(3, 1)
-        fin(3, 0)
-        st(3)
+        t2c(5)
+        vt(7)
         val(2, 0)
-        t2(7)
-        t2(6)
-        t2c(7)
-        fin(2, 1)
-        val(5, 1)
-        val(5, 0)
+        val(2, 1)
+        val(3, 1)
+        t1c(6)
+        val(3, 0)
+        t1c(7)
+        fin(4, 1)
+        st(4)
         fin(2, 0)
+        fin(2, 1)
         st(2)
-        qu(7)
+        qu(5)
+        t2(6)
         t2c(6)
-        gate(6, 0)
-        gate(7, 1)
-        silu(7, 1)
-        fin(5, 1)
-        fin(5, 0)
-        st(5)
-        val(7, 0)
+        fin(3, 0)
+        fin(3, 1)
+        st(3)
         qu(6)
-        fin(7, 0)
-        sth(7, 0)
-        val(7, 1)
-        silu(6, 0)
+        t2(7)
+        val(5, 0)
+        fin(5, 0)
+        val(5, 1)
+        t2c(7)
+        qu(7)
         gate(6, 1)
+        gate(7, 1)
+        val(7, 1)
+        fin(5, 1)
+        st(5)
+        val(6, 1)
+        silu(7, 1)
         fin(7, 1)
         sth(7, 1)
         silu(6, 1)
-        val(6, 0)
-        val(6, 1)
-        fin(6, 0)
-        sth(6, 0)
         fin(6, 1)
         sth(6, 1)
+        gate(6, 0)
+        val(7, 0)
+        val(6, 0)
+        silu(6, 0)
+        fin(7, 0)
+        sth(7, 0)
+        fin(6, 0)
+        sth(6, 0)

@@ -87,8 +87,12 @@ def tile_productkeysoftmemoryplus_w4_kernel(
         for c, tiles in enumerate(BATCHES):
             left.append(keep.tile([P, 4 * len(tiles), Q, N], F32, name=f"left{c}"))
             left_c.append(keep.tile([P, 4 * len(tiles), N], F32, name=f"left_c{c}"))
-            right.append(keep.tile([P, 4 * len(tiles), 8, N], F32, name=f"right{c}"))
-            (nc.gpsimd if c == 2 else nc.vector).memset(right[c][:], 0.0)
+            if c < 2:
+                right.append(keep.tile([P, 12, 8, N], F32, name=f"right{c}"))
+                for g in range(0, 12, 2):
+                    nc.gpsimd.memset(right[c][:, g : g + 2], 0.0)
+            else:
+                right.append(right[0])
         for q in range(Q):
             nc.sync.dma_start(out=gain[32 * q : 32 * q + 32, :], in_=slot_gain.rearrange("(i j) -> i j", j=N))
 
@@ -195,7 +199,7 @@ def tile_productkeysoftmemoryplus_w4_kernel(
             )
 
         def neg(n):
-            nc.vector.tensor_scalar(out=S["top", n][:], in0=S["top", n][:], scalar1=-1.0, scalar2=None, op0=MUL)
+            nc.scalar.activation(out=S["top", n][:], in_=S["top", n][:], func=COPY, scale=-1.0)
 
         def ex(n):
             ps, e, top, z = S["sc", n], S["e", n], S["top", n], S["z", n]
@@ -235,7 +239,7 @@ def tile_productkeysoftmemoryplus_w4_kernel(
 
         def rd(c, r):
             rows = park_rows(BATCHES[c][0], len(BATCHES[c])).rearrange("(g r) (c a n) -> a (r c) g n", r=8, a=2, n=N)
-            nc.sync.dma_start(out=right[c][16 * r : 16 * r + 16, :, r, :], in_=rows[1][16 * r : 16 * r + 16])
+            nc.sync.dma_start(out=right[c][16 * r : 16 * r + 16, 0 : 4 * len(BATCHES[c]), r, :], in_=rows[1][16 * r : 16 * r + 16])
 
         def lm(c, q, eng="V"):
             if eng == "V":
@@ -327,285 +331,285 @@ def tile_productkeysoftmemoryplus_w4_kernel(
             sl = slice(512 * b, 512 * b + 512)
             nc.sync.dma_start(out=out[128 * n : 128 * n + 128, sl], in_=S["gate", n][:, sl])
 
-        xs(1)
         xs(0)
-        xt(1)
-        xc(1)
-        xs(3)
-        qx(1)
+        xs(1)
         xt(0)
+        xs(3)
         xc(0)
-        xs(2)
         qx(0)
-        sc(1)
+        xs(2)
+        xt(1)
         xt(3)
         sc(0)
+        xc(1)
+        xt(2)
+        qx(1)
+        mx(0)
         xc(3)
-        mx(1)
+        neg(0)
         xs(4)
         qx(3)
-        xt(2)
-        xc(2)
-        xt(4)
-        mx(0)
-        neg(1)
-        xs(5)
-        neg(0)
-        ex(1)
-        sc(3)
-        xc(4, "V")
-        qx(2)
-        consts()
-        nz(1)
-        mx(3)
+        sc(1)
         ex(0)
+        mx(1)
+        xc(2)
+        xs(5)
+        consts()
+        nz(0)
+        sc(3)
+        xt(4)
+        qx(2)
+        neg(1)
+        ex(1)
+        nr(0)
+        xc(4)
+        mx(3)
+        nz(1)
+        norm(0)
+        neg(3)
         nr(1)
         xt(5)
+        park(0)
         qx(4)
-        nz(0)
-        neg(3)
-        sc(2)
         norm(1)
-        nr(0)
-        xc(5)
+        sc(2)
         sc(4)
         mx(2)
-        norm(0)
-        park(1)
-        park(0)
-        rd(0, 5)
-        neg(2)
-        qx(5)
         ex(3)
+        xc(5, "V")
         mx(4)
-        sc(5)
-        neg(4)
-        ex(2)
-        gate(2, 1)
-        gate(5, 1)
-        mx(5)
-        nz(2)
+        qx(5)
         nz(3)
-        ld(0)
-        neg(5)
-        gate(0, 1)
-        gate(5, 0)
-        xs(7)
-        ex(4)
-        nz(4)
-        rd(0, 4)
-        nr(2)
-        xt(7)
-        xs(6)
-        ex(5)
-        nz(5)
-        nr(5)
-        rd(0, 3)
-        norm(2)
-        silu(2, 1)
-        gate(1, 0)
-        rd(0, 1)
-        silu(5, 1)
-        nr(4)
-        gate(0, 0)
-        xc(7, "V")
-        silu(0, 1)
-        xt(6)
-        rd(0, 0)
-        norm(5)
-        norm(4)
-        silu(1, 0)
-        nr(3)
-        lm(0, 1)
-        gate(1, 1)
-        silu(5, 0)
-        norm(3)
-        rd(0, 7)
-        rd(0, 6)
+        neg(2)
+        park(1)
         rd(0, 2)
-        qx(7)
-        park(2)
+        sc(5)
+        nr(3)
+        rd(0, 3)
+        ex(2)
+        mx(5)
+        neg(4)
+        nz(2)
+        gate(1, 0)
+        rd(0, 4)
+        gate(2, 1)
+        ex(4)
+        neg(5)
+        xs(7)
+        rd(0, 7)
+        rd(0, 1)
+        nr(2)
+        nz(4)
+        rd(0, 0)
+        rd(0, 6)
+        ex(5)
+        gate(0, 0)
+        nr(4)
+        xs(6)
+        ld(0)
+        gate(0, 1)
+        rd(0, 5)
+        gate(5, 0)
+        norm(3)
+        xt(7)
+        norm(4)
+        xt(6)
+        silu(1, 0)
+        norm(2)
         park(4)
-        gate(7, 0)
-        silu(7, 0)
-        sc(7)
-        xc(6, "V")
-        lm(0, 3)
-        qx(6)
-        sc(6)
-        lm(0, 0)
+        xc(7, "V")
         park(3)
+        gate(5, 1)
+        lm(0, 1)
+        nz(5)
+        silu(2, 1)
         lm(0, 2)
-        ld(1)
-        rd(1, 5)
-        prod(1, 1)
-        rd(1, 3)
+        silu(0, 0)
+        qx(7)
+        nr(5)
+        park(2)
+        gate(1, 1)
+        silu(0, 1)
+        gate(7, 0)
+        silu(1, 1)
+        sc(7)
+        lm(0, 3)
+        lm(0, 0)
+        mx(7)
+        silu(5, 0)
+        rd(1, 6)
         rd(1, 2)
         rd(1, 4)
-        silu(0, 0)
-        mx(7)
-        mx(6)
-        neg(6)
-        silu(1, 1)
-        neg(7)
-        ex(7)
-        ex(6)
-        prod(0, 0)
-        rd(1, 1)
-        gn(1, 1)
-        gn(0, 0)
-        nz(7)
-        park(5)
-        lm(1, 0, "S")
         prod(1, 0)
+        silu(5, 1)
+        rd(1, 1)
+        silu(7, 0)
+        neg(7)
+        prod(1, 1)
+        xc(6, "V")
+        qx(6)
         gn(1, 0)
-        prod(0, 1)
-        lm(1, 2, "S")
-        gate(2, 0)
-        rd(1, 6)
-        gate(3, 0)
-        nr(7)
-        lm(1, 1, "S")
-        nz(6)
-        nr(6)
-        gn(0, 1)
-        silu(2, 0)
-        lm(1, 3)
-        rd(1, 7)
-        norm(6)
+        sc(6)
+        gn(1, 1)
+        ld(1)
+        mx(6)
+        prod(0, 0)
+        gn(0, 0)
         rd(1, 0)
-        norm(7)
-        park(7)
-        vt(0)
-        t1c(0, "V")
-        gate(3, 1)
-        vt(1)
+        ex(7)
+        neg(6)
+        prod(0, 1)
+        ex(6)
+        nz(7)
+        rd(1, 7)
+        lm(1, 3, "S")
+        norm(5)
         gate(4, 0)
-        prod(2, 0)
-        prod(2, 1)
-        silu(4, 0)
-        gn(2, 0)
-        t2(0)
-        park(6)
-        t1c(1)
-        t2c(0, "V")
-        silu(3, 0)
-        prod(4, 0)
-        qu(0)
-        t2(1)
-        rd(2, 2)
+        nr(7)
+        rd(1, 5)
+        lm(1, 2)
+        rd(1, 3)
+        lm(1, 0)
+        nz(6)
+        gate(6, 1)
+        norm(7)
+        nr(6)
+        gate(6, 0)
+        park(5)
+        gate(3, 1)
+        lm(1, 1)
+        gn(0, 1)
+        norm(6)
         silu(3, 1)
-        rd(2, 4)
-        gn(4, 0)
-        ld(2)
-        t2c(1)
+        vt(0)
+        silu(4, 0)
+        prod(4, 0)
+        vt(1)
         prod(4, 1)
-        val(0, 1)
-        lm(2, 1, "S")
-        val(0, 0)
-        rd(2, 6)
-        gn(2, 1)
-        qu(1)
-        gn(4, 1)
-        lm(2, 2, "S")
+        park(6)
+        park(7)
+        silu(6, 1)
+        t1c(1)
+        ld(2)
         rd(2, 1)
-        rd(2, 7)
-        fin(0, 1)
-        val(1, 1)
-        fin(0, 0)
-        st(0)
-        val(1, 0)
-        rd(2, 3)
-        rd(2, 5)
-        fin(1, 1)
-        fin(1, 0)
-        st(1)
-        lm(2, 0, "S")
-        prod(3, 1)
-        lm(2, 3, "S")
-        rd(2, 0)
+        silu(6, 0)
+        gn(4, 0)
+        t1c(0, "V")
+        rd(2, 2)
         prod(3, 0)
+        t2(0)
+        gn(4, 1)
         vt(4)
-        vt(2)
-        gn(3, 1)
-        t1c(2)
-        gn(3, 0)
-        prod(5, 0)
-        prod(5, 1)
-        t2(2)
-        vt(3)
+        prod(2, 1)
+        prod(3, 1)
         t1c(4)
-        t1c(3, "V")
-        gn(5, 0)
         t2(4)
-        t2c(2)
-        prod(6, 1)
-        gn(5, 1)
-        prod(6, 0)
-        qu(2)
-        t2(3)
-        vt(5)
-        gn(6, 1)
+        rd(2, 5)
+        rd(2, 6)
+        t2c(0, "V")
+        rd(2, 4)
+        gn(3, 0)
+        gn(2, 1)
+        rd(2, 3)
+        qu(0)
+        rd(2, 0)
+        rd(2, 7)
+        gn(3, 1)
         t2c(4)
-        t1c(5)
-        gn(6, 0)
-        prod(7, 0)
-        t2(5)
-        prod(7, 1)
+        lm(2, 3, "S")
         qu(4)
-        vt(6)
-        val(4, 0)
-        gn(7, 0)
-        t2c(3)
-        qu(3)
+        lm(2, 2, "S")
+        lm(2, 0, "S")
+        t2(1)
+        prod(2, 0)
+        vt(3)
+        gn(2, 0)
         gate(4, 1)
+        val(4, 0)
         val(4, 1)
-        gn(7, 1)
         silu(4, 1)
+        t2c(1)
         fin(4, 0)
-        t2c(5)
-        vt(7)
-        val(2, 0)
-        val(2, 1)
-        val(3, 1)
-        t1c(6)
-        val(3, 0)
-        t1c(7)
+        gate(2, 0)
+        lm(2, 1, "S")
+        t1c(3)
+        val(0, 1)
+        prod(5, 1)
         fin(4, 1)
         st(4)
+        prod(5, 0)
+        qu(1)
+        vt(2)
+        gn(5, 1)
+        fin(0, 1)
+        t1c(2)
+        t2(3)
+        gn(5, 0)
+        prod(7, 1)
+        silu(2, 0)
+        t2c(3, "V")
+        vt(5)
+        t1c(5)
+        prod(7, 0)
+        t2(2)
+        gn(7, 1)
+        prod(6, 1)
+        gn(7, 0)
+        vt(7)
+        qu(3)
+        t2(5)
+        t2c(2)
+        prod(6, 0)
+        gn(6, 1)
+        qu(2)
+        t2c(5)
+        val(0, 0)
+        gate(3, 0)
+        gn(6, 0)
+        val(3, 1)
+        silu(3, 0)
+        fin(0, 0)
+        st(0)
+        vt(6)
+        val(3, 0)
+        fin(3, 1)
+        fin(3, 0)
+        st(3)
+        val(1, 1)
+        fin(1, 1)
+        val(1, 0)
+        t1c(7)
+        t1c(6)
+        fin(1, 0)
+        st(1)
+        qu(5)
+        val(2, 0)
+        t2(7)
         fin(2, 0)
+        t2(6)
+        t2c(7)
+        val(2, 1)
+        val(5, 0)
+        gate(7, 1)
+        t2c(6)
+        qu(7)
         fin(2, 1)
         st(2)
-        qu(5)
-        t2(6)
-        t2c(6)
-        fin(3, 0)
-        fin(3, 1)
-        st(3)
-        qu(6)
-        t2(7)
-        val(5, 0)
-        fin(5, 0)
-        val(5, 1)
-        t2c(7)
-        qu(7)
-        gate(6, 1)
-        gate(7, 1)
+        val(7, 0)
         val(7, 1)
-        fin(5, 1)
-        st(5)
-        val(6, 1)
+        qu(6)
         silu(7, 1)
+        val(5, 1)
+        fin(5, 0)
+        sth(5, 0)
+        fin(7, 0)
         fin(7, 1)
-        sth(7, 1)
-        silu(6, 1)
+        st(7)
+        val(6, 1)
+        fin(5, 1)
+        sth(5, 1)
         fin(6, 1)
         sth(6, 1)
-        gate(6, 0)
-        val(7, 0)
         val(6, 0)
-        silu(6, 0)
-        fin(7, 0)
-        sth(7, 0)
         fin(6, 0)
         sth(6, 0)

from contextlib import ExitStack

import concourse.mybir as mybir
from concourse.masks import make_identity

T, D, H, N = 1024, 1024, 4, 32
C = H * 2 * N
SLOTS = N * N
FLOPS = 2 * T * D * C + 2 * T * SLOTS * D + 2 * T * D * D

P = 128
PACK = 4
PASSES = 2
NT = 8
Q = 4
BATCHES = ((0, 1), (2, 3, 4), (5, 6, 7))

F32 = mybir.dt.float32
BF16 = mybir.dt.bfloat16
I32 = mybir.dt.int32
U32 = mybir.dt.uint32
U8 = mybir.dt.uint8
FP8 = mybir.dt.float8_e4m3fn
E4M3X4 = mybir.dt.float8_e4m3fn_x4
E2M1X4 = mybir.dt.float4_e2m1fn_x4
ADD = mybir.AluOpType.add
SUB = mybir.AluOpType.subtract
MUL = mybir.AluOpType.mult
MAX = mybir.AluOpType.max
AX = mybir.AxisListType.X
EXP = mybir.ActivationFunctionType.Exp
COPY = mybir.ActivationFunctionType.Copy
SILU = mybir.ActivationFunctionType.Silu


def tile_productkeysoftmemoryplus_w4_kernel(
    tc, x_bytes, x_scale, wk_words, wk_scales, slot_gain, values_words, values_scales, wg_words, wg_scales, out
):
    nc = tc.nc
    with ExitStack() as ctx:
        keep = ctx.enter_context(tc.tile_pool(name="keep", bufs=1))
        work = ctx.enter_context(tc.tile_pool(name="work", bufs=6))
        pst = ctx.enter_context(tc.psum_pool(name="pst", bufs=2))
        psm = ctx.enter_context(tc.psum_pool(name="psm", bufs=6))
        ctx.enter_context(tc.manual_schedule())
        S = {}

        warm = keep.tile([P, 1], F32, name="warm")
        nc.vector.memset(warm[:], 0.0)
        nc.scalar.activation(out=warm[:], in_=warm[:], func=EXP)

        x_view = x_bytes.rearrange("(n p) d -> p n d", p=P)
        xb = [keep.tile([P, k, D], U8, name=f"xb{k}_{n}", align_bytes=64) for n, k in ((0, 1), (1, 3), (4, 4))]
        X_AT = {n: (xb[0] if n == 0 else xb[1] if n < 4 else xb[2], n - (0 if n == 0 else 1 if n < 4 else 4)) for n in range(NT)}
        scale_col = keep.tile([P, 8], F32, name="scale_col")
        nc.sync.dma_start(out=scale_col[:], in_=x_scale.rearrange("o (m p) -> p (o m)", p=P))
        nc.sync.dma_start(out=xb[0][:], in_=x_view[:, 0:1, :])
        nc.sync.dma_start(out=xb[1][:], in_=x_view[:, 1:4, :])

        ident = keep.tile([P, P], F32, name="ident", align_bytes=64)
        make_identity(nc, ident[:])

        def load_weight(words, scales, n, name):
            w = keep.tile([P, PASSES, 2 * n], U8, name=name + "_w", align_bytes=64)
            sc = keep.tile([P, PASSES, n], U8, name=name + "_s", align_bytes=64)
            nc.vector.memset(sc[:].rearrange("p g n -> p (g n)").bitcast(I32), 0)
            nc.sync.dma_start(
                out=w[:].rearrange("p g n -> p (g n)").bitcast(I32).rearrange("p (g n) -> p g n", g=PASSES),
                in_=words.rearrange("g p n -> (g p) n").bitcast(I32).rearrange("(g p) n -> p g n", g=PASSES),
            )
            s32 = sc[:].rearrange("p g n -> p (g n)").bitcast(I32).rearrange("p (g n) -> p g n", g=PASSES)
            src = scales.rearrange("g r n -> (g r) n").bitcast(I32).rearrange("(g r) n -> r g n", g=PASSES)
            for quad in range(4):
                nc.sync.dma_start(out=s32[32 * quad : 32 * quad + 4], in_=src[4 * quad : 4 * quad + 4])
            return w, sc

        wk_w, wk_s = load_weight(wk_words, wk_scales, C, "wk")
        wg_w, wg_s = load_weight(wg_words, wg_scales, D, "wg")
        nc.sync.dma_start(out=xb[2][:], in_=x_view[:, 4:8, :])
        gain = keep.tile([P, N], BF16, name="gain")
        v_w, v_s = load_weight(values_words, values_scales, D, "vl")

        mask = keep.tile([P, Q], F32, name="mask")
        perm = keep.tile([P, P], F32, name="perm", align_bytes=64)
        place = {n: (c, 4 * k) for c, tiles in enumerate(BATCHES) for k, n in enumerate(tiles)}
        left, left_c, right = [], [], []
        for c, tiles in enumerate(BATCHES):
            left.append(keep.tile([P, 4 * len(tiles), Q, N], F32, name=f"left{c}"))
            left_c.append(keep.tile([P, 4 * len(tiles), N], F32, name=f"left_c{c}"))
            if c < 2:
                right.append(keep.tile([P, 12, 8, N], F32, name=f"right{c}"))
                for g in range(0, 12, 2):
                    nc.gpsimd.memset(right[c][:, g : g + 2], 0.0)
            else:
                right.append(right[0])
        for q in range(Q):
            nc.sync.dma_start(out=gain[32 * q : 32 * q + 32, :], in_=slot_gain.rearrange("(i j) -> i j", j=N))

        scl = keep.tile([P, D], F32, name="scl")
        for b in range(2):
            ps = psm.tile([P, 512], F32, name="mm")
            for m in range(4):
                nc.tensor.transpose(
                    ps[:, 128 * m : 128 * m + 128], scale_col[:, 4 * b + m : 4 * b + m + 1].to_broadcast([P, P]), ident[:]
                )
            if b == 0:
                nc.scalar.copy(out=scl[:, 0:512], in_=ps[:])
            else:
                nc.vector.tensor_copy(out=scl[:, 512:1024], in_=ps[:])

        def consts():
            nc.vector.tensor_reduce(
                out=mask[:],
                in_=ident[:].rearrange("p (r q h) -> p q r h", q=Q, h=H),
                axis=mybir.AxisListType.XY,
                op=ADD,
            )
            nc.vector.tensor_copy(
                out=perm[:].rearrange("p (r q) -> p r q", q=Q), in_=ident[:].rearrange("p (q r) -> p r q", q=Q)
            )

        def xs(n):
            t = work.tile([P, D], BF16, name="xs", align_bytes=64)
            src, k = X_AT[n]
            nc.vector.tensor_tensor(out=t[:], in0=src[:, k, :].bitcast(FP8), in1=scl[:], op=MUL)
            S["xs", n] = t

        def xt(n):
            xw = S["xs", n][:].bitcast(F32)
            ps = pst.tile([P, PASSES, 2, P], F32, name="tp")
            for g in range(PASSES):
                for u in range(2):
                    nc.tensor.transpose(ps[:, g, u, :], xw[:, 256 * g + u : 256 * (g + 1) : 2], ident[:])
            S["xt", n] = ps

        def copy_out(eng, dst, src):
            if eng == "V":
                nc.vector.tensor_copy(out=dst, in_=src)
            else:
                nc.scalar.copy(out=dst, in_=src)

        def interleave(eng, ps):
            t = work.tile([P, PASSES, P, PACK], BF16, name="xg", align_bytes=64)
            copy_out(
                eng,
                t[:].rearrange("p g r t -> p (g r t)").bitcast(F32).rearrange("p (g r u) -> p g r u", g=PASSES, u=2),
                ps[:].rearrange("p g u r -> p g r u"),
            )
            return t

        def xc(n, eng="S"):
            S["xg", n] = interleave(eng, S["xt", n])

        def quant(src, key):
            nm = key[0] + str(key[1])
            c = keep.tile([P, PASSES, P], U32, name="c_" + nm, align_bytes=64)
            sc = keep.tile([P, PASSES, P], U8, name="s_" + nm, align_bytes=64)
            nc.vector.quantize_mx(
                out=c[:].rearrange("p g r -> p (g r)").bitcast(E4M3X4),
                scales=sc[:].rearrange("p g r -> p (g r)"),
                in_=src[:].rearrange("p g r t -> p (g r t)"),
            )
            S[key] = (c, sc)

        def qx(n):
            quant(S["xg", n], ("x", n))

        def mm(ps, key, w, wsc, n0, n):
            codes, scales = S[key]
            for g in range(PASSES):
                nc.tensor.matmul_mx(
                    out=ps,
                    lhsT=codes[:, g, :].bitcast(E4M3X4),
                    lhsT_scale=scales[:, g, :],
                    rhs=w[:, g, 2 * n0 : 2 * (n0 + n)].bitcast(E2M1X4),
                    rhs_scale=wsc[:, g, n0 : n0 + n],
                    start=(g == 0),
                    stop=(g == PASSES - 1),
                )

        for n in range(NT):
            S["e", n] = keep.tile([P, H, 2, N], F32, name=f"e{n}")
            S["z", n] = keep.tile([P, H, 2], F32, name=f"z{n}")
            S["top", n] = keep.tile([P, H, 2], F32, name=f"top{n}")
            S["rz", n] = keep.tile([P, H], F32, name=f"rz{n}")

        def sc(n):
            ps = psm.tile([P, C], F32, name="mm")
            for n0 in (0, 128):
                mm(ps[:, n0 : n0 + 128], ("x", n), wk_w, wk_s, n0, 128)
            S["sc", n] = ps

        def mx(n):
            nc.vector.tensor_reduce(
                out=S["top", n][:].rearrange("p h a -> p (h a)"),
                in_=S["sc", n][:].rearrange("p (c n) -> p c n", n=N),
                axis=AX,
                op=MAX,
            )

        def neg(n):
            nc.scalar.activation(out=S["top", n][:], in_=S["top", n][:], func=COPY, scale=-1.0)

        def ex(n):
            ps, e, top, z = S["sc", n], S["e", n], S["top", n], S["z", n]
            for h in range(H):
                for a in range(2):
                    k = 2 * h + a
                    nc.scalar.activation(
                        out=e[:, h, a, :],
                        in_=ps[:, N * k : N * k + N],
                        func=EXP,
                        bias=top[:, h, a : a + 1],
                        accum_out=z[:, h, a : a + 1],
                    )

        def nz(n):
            z = S["z", n]
            nc.vector.tensor_tensor(out=S["rz", n][:], in0=z[:, :, 0], in1=z[:, :, 1], op=MUL)

        def nr(n):
            nc.vector.reciprocal(out=S["rz", n][:], in_=S["rz", n][:])

        def norm(n):
            first = S["e", n][:, :, 0, :]
            nc.vector.tensor_tensor(out=first, in0=first, in1=S["rz", n][:].unsqueeze(2).to_broadcast([P, H, N]), op=MUL)

        def park_rows(n, k):
            return out[768 + 32 * n : 768 + 32 * (n + k), :]

        def park(n):
            nc.sync.dma_start(
                out=park_rows(n, 1).rearrange("r (q f) -> (r q) f", q=Q), in_=S["e", n][:].rearrange("p h a n -> p (h a n)")
            )

        def ld(c):
            rows = park_rows(BATCHES[c][0], len(BATCHES[c])).rearrange("(g r) (c a n) -> a (r c) g n", r=8, a=2, n=N)
            nc.sync.dma_start(out=left_c[c][:], in_=rows[0])

        def rd(c, r):
            rows = park_rows(BATCHES[c][0], len(BATCHES[c])).rearrange("(g r) (c a n) -> a (r c) g n", r=8, a=2, n=N)
            nc.sync.dma_start(out=right[c][16 * r : 16 * r + 16, 0 : 4 * len(BATCHES[c]), r, :], in_=rows[1][16 * r : 16 * r + 16])

        def lm(c, q, eng="V"):
            if eng == "V":
                nc.vector.tensor_scalar(out=left[c][:, :, q, :], in0=left_c[c][:], scalar1=mask[:, q : q + 1], scalar2=None, op0=MUL)
            elif eng == "G":
                nc.gpsimd.tensor_scalar(
                    out=left[c][:, :, q, :], in0=left_c[c][:], scalar1=mask[:, q : q + 1], scalar2=0.0, op0=MUL, op1=ADD
                )
            else:
                nc.scalar.activation(out=left[c][:, :, q, :], in_=left_c[c][:], func=COPY, scale=mask[:, q : q + 1])

        def gate(n, b):
            if ("gate", n) not in S:
                S["gate", n] = keep.tile([P, D], F32, name=f"gate{n}")
            ps = psm.tile([P, 512], F32, name="mm")
            mm(ps[:], ("x", n), wg_w, wg_s, 512 * b, 512)
            S["a", n, b] = ps

        def silu(n, b):
            nc.scalar.activation(out=S["gate", n][:, 512 * b : 512 * b + 512], in_=S["a", n, b][:], func=SILU)

        for n in range(NT):
            S["wt", n] = keep.tile([P, 16, 32, 2], BF16, name=f"wt{n}", align_bytes=64)
            S["u1", n] = keep.tile([P, 2, 32, 8], F32, name=f"u1{n}", align_bytes=64)

        def prod(n, b):
            ps = psm.tile([P, 2, 8 * N], F32, name="mm")
            c, g0 = place[n]
            for k in range(2):
                grp = g0 + 2 * b + k
                nc.tensor.matmul(
                    out=ps[:, k, :],
                    lhsT=left[c][:, grp, :, :].rearrange("p q n -> p (q n)"),
                    rhs=right[c][:, grp, :, :].rearrange("p r n -> p (r n)"),
                    start=True,
                    stop=True,
                )
            S["pr", n, b] = ps

        def gn(n, b):
            nc.vector.tensor_tensor(
                out=S["wt", n][:, :, 16 * b : 16 * b + 16, :],
                in0=S["pr", n, b][:].rearrange("p k (r w e) -> p w (k r) e", r=8, e=2),
                in1=gain[:].rearrange("p (w e) -> p w e", e=2).unsqueeze(2).to_broadcast([P, 16, 16, 2]),
                op=MUL,
            )

        def vt(n):
            S["ut", n] = work.tile([P, 16, 32], F32, name="ut", align_bytes=64)
            nc.vector.transpose(
                out=S["ut", n][:].rearrange("p w i -> p (w i)"),
                in_=S["wt", n][:].rearrange("p w r e -> p (w r e)").bitcast(F32),
            )

        def t1c(n, eng="S"):
            src = S["ut", n][:].rearrange("p (a c u) i -> p u a i c", a=2, u=2)
            dst = S["u1", n][:].rearrange("p u i (a c) -> p u a i c", a=2)
            for u in range(2):
                copy_out(eng, dst[:, u], src[:, u])

        def t2(n):
            ps = pst.tile([P, PASSES, 2, P], F32, name="tp")
            for g in range(PASSES):
                for u in range(2):
                    nc.tensor.transpose(
                        ps[:, g, u, :], S["u1", n][:, u, 16 * g : 16 * g + 16, :].rearrange("p i j -> p (i j)"), perm[:]
                    )
            S["t2", n] = ps

        def t2c(n, eng="S"):
            S["ug", n] = interleave(eng, S["t2", n])

        def qu(n):
            quant(S["ug", n], ("u", n))

        def val(n, b):
            ps = psm.tile([P, 512], F32, name="mm")
            mm(ps[:], ("u", n), v_w, v_s, 512 * b, 512)
            S["mem", n, b] = ps

        def fin(n, b):
            g = S["gate", n][:, 512 * b : 512 * b + 512]
            nc.vector.tensor_tensor(out=g, in0=S["mem", n, b][:], in1=g, op=MUL)

        def st(n):
            nc.sync.dma_start(out=out[128 * n : 128 * n + 128, :], in_=S["gate", n][:])

        def sth(n, b):
            sl = slice(512 * b, 512 * b + 512)
            nc.sync.dma_start(out=out[128 * n : 128 * n + 128, sl], in_=S["gate", n][:, sl])

        xs(0)
        xs(1)
        xt(0)
        xs(3)
        xc(0)
        qx(0)
        xs(2)
        xt(1)
        xt(3)
        sc(0)
        xc(1)
        xt(2)
        qx(1)
        mx(0)
        xc(3)
        neg(0)
        xs(4)
        qx(3)
        sc(1)
        ex(0)
        mx(1)
        xc(2)
        xs(5)
        consts()
        nz(0)
        sc(3)
        xt(4)
        qx(2)
        neg(1)
        ex(1)
        nr(0)
        xc(4)
        mx(3)
        nz(1)
        norm(0)
        neg(3)
        nr(1)
        xt(5)
        park(0)
        qx(4)
        norm(1)
        sc(2)
        sc(4)
        mx(2)
        ex(3)
        xc(5, "V")
        mx(4)
        qx(5)
        nz(3)
        neg(2)
        park(1)
        rd(0, 2)
        sc(5)
        nr(3)
        rd(0, 3)
        ex(2)
        mx(5)
        neg(4)
        nz(2)
        gate(1, 0)
        rd(0, 4)
        gate(2, 1)
        ex(4)
        neg(5)
        xs(7)
        rd(0, 7)
        rd(0, 1)
        nr(2)
        nz(4)
        rd(0, 0)
        rd(0, 6)
        ex(5)
        gate(0, 0)
        nr(4)
        xs(6)
        ld(0)
        gate(0, 1)
        rd(0, 5)
        gate(5, 0)
        norm(3)
        xt(7)
        norm(4)
        xt(6)
        silu(1, 0)
        norm(2)
        park(4)
        xc(7, "V")
        park(3)
        gate(5, 1)
        lm(0, 1)
        nz(5)
        silu(2, 1)
        lm(0, 2)
        silu(0, 0)
        qx(7)
        nr(5)
        park(2)
        gate(1, 1)
        silu(0, 1)
        gate(7, 0)
        silu(1, 1)
        sc(7)
        lm(0, 3)
        lm(0, 0)
        mx(7)
        silu(5, 0)
        rd(1, 6)
        rd(1, 2)
        rd(1, 4)
        prod(1, 0)
        silu(5, 1)
        rd(1, 1)
        silu(7, 0)
        neg(7)
        prod(1, 1)
        xc(6, "V")
        qx(6)
        gn(1, 0)
        sc(6)
        gn(1, 1)
        ld(1)
        mx(6)
        prod(0, 0)
        gn(0, 0)
        rd(1, 0)
        ex(7)
        neg(6)
        prod(0, 1)
        ex(6)
        nz(7)
        rd(1, 7)
        lm(1, 3, "S")
        norm(5)
        gate(4, 0)
        nr(7)
        rd(1, 5)
        lm(1, 2)
        rd(1, 3)
        lm(1, 0)
        nz(6)
        gate(6, 1)
        norm(7)
        nr(6)
        gate(6, 0)
        park(5)
        gate(3, 1)
        lm(1, 1)
        gn(0, 1)
        norm(6)
        silu(3, 1)
        vt(0)
        silu(4, 0)
        prod(4, 0)
        vt(1)
        prod(4, 1)
        park(6)
        park(7)
        silu(6, 1)
        t1c(1)
        ld(2)
        rd(2, 1)
        silu(6, 0)
        gn(4, 0)
        t1c(0, "V")
        rd(2, 2)
        prod(3, 0)
        t2(0)
        gn(4, 1)
        vt(4)
        prod(2, 1)
        prod(3, 1)
        t1c(4)
        t2(4)
        rd(2, 5)
        rd(2, 6)
        t2c(0, "V")
        rd(2, 4)
        gn(3, 0)
        gn(2, 1)
        rd(2, 3)
        qu(0)
        rd(2, 0)
        rd(2, 7)
        gn(3, 1)
        t2c(4)
        lm(2, 3, "S")
        qu(4)
        lm(2, 2, "S")
        lm(2, 0, "S")
        t2(1)
        prod(2, 0)
        vt(3)
        gn(2, 0)
        gate(4, 1)
        val(4, 0)
        val(4, 1)
        silu(4, 1)
        t2c(1)
        fin(4, 0)
        gate(2, 0)
        lm(2, 1, "S")
        t1c(3)
        val(0, 1)
        prod(5, 1)
        fin(4, 1)
        st(4)
        prod(5, 0)
        qu(1)
        vt(2)
        gn(5, 1)
        fin(0, 1)
        t1c(2)
        t2(3)
        gn(5, 0)
        prod(7, 1)
        silu(2, 0)
        t2c(3, "V")
        vt(5)
        t1c(5)
        prod(7, 0)
        t2(2)
        gn(7, 1)
        prod(6, 1)
        gn(7, 0)
        vt(7)
        qu(3)
        t2(5)
        t2c(2)
        prod(6, 0)
        gn(6, 1)
        qu(2)
        t2c(5)
        val(0, 0)
        gate(3, 0)
        gn(6, 0)
        val(3, 1)
        silu(3, 0)
        fin(0, 0)
        st(0)
        vt(6)
        val(3, 0)
        fin(3, 1)
        fin(3, 0)
        st(3)
        val(1, 1)
        fin(1, 1)
        val(1, 0)
        t1c(7)
        t1c(6)
        fin(1, 0)
        st(1)
        qu(5)
        val(2, 0)
        t2(7)
        fin(2, 0)
        t2(6)
        t2c(7)
        val(2, 1)
        val(5, 0)
        gate(7, 1)
        t2c(6)
        qu(7)
        fin(2, 1)
        st(2)
        val(7, 0)
        val(7, 1)
        qu(6)
        silu(7, 1)
        val(5, 1)
        fin(5, 0)
        sth(5, 0)
        fin(7, 0)
        fin(7, 1)
        st(7)
        val(6, 1)
        fin(5, 1)
        sth(5, 1)
        fin(6, 1)
        sth(6, 1)
        val(6, 0)
        fin(6, 0)
        sth(6, 0)
